import numpy as np
import ml_dtypes


def mxq(x, axis, fmt="e4m3"):
    dtype, down = {"e4m3": (ml_dtypes.float8_e4m3fn, 7), "e5m2": (ml_dtypes.float8_e5m2, 14)}[fmt]
    v = np.moveaxis(np.asarray(x, np.float32).astype(ml_dtypes.bfloat16).astype(np.float64), axis, -1)
    blocks = v.reshape(v.shape[:-1] + (-1, 32))
    amax = np.abs(blocks).max(-1, keepdims=True)
    byte = np.maximum(np.where(amax > 0, np.frexp(amax)[1] - 1 + 127, 0) - down, 1)
    scale = np.exp2(byte - 127.0)
    codes = (blocks / scale).astype(np.float32).astype(dtype).astype(np.float64)
    return np.moveaxis((codes * scale).reshape(v.shape), -1, axis)


WIDE = False


def mx_kscale(k):
    if not WIDE:
        return np.ones(k)
    levels = np.array([10, -10, 5, -5, 0])
    if k % 512:
        return np.exp2(np.random.permutation(np.resize(levels, k // 32))).repeat(32)
    a = np.empty((k // 512, 16))
    for p in range(k // 512):
        a[p, :8] = np.random.permutation(np.resize(levels, 8))
        for g in range(8):
            far = levels[np.abs(levels - a[p, g]) >= 10]
            a[p, g + 8] = far[np.random.randint(len(far))]
    return np.exp2(a.ravel()).repeat(32)


def f64(x):
    return np.asarray(x).astype(np.float64)


def striped(idx):
    return np.tile(np.asarray(idx).reshape(-1, 16).T, (8, 1)).astype(np.uint16)


def unstriped(offs):
    return offs[:16].T.reshape(-1).astype(np.int64)


E2M1 = np.array([0.0, 0.5, 1.0, 1.5, 2.0, 3.0, 4.0, 6.0, -0.0, -0.5, -1.0, -1.5, -2.0, -3.0, -4.0, -6.0])


def pack_weight(w, fmt):
    k, n = w.shape
    w = f64(np.asarray(w, np.float32).astype(ml_dtypes.bfloat16)).reshape(k // 32, 32, n)
    amax = np.abs(w).max(1)
    if fmt == "e4m3":
        byte = np.frexp(amax)[1] - 1 + 127 - 7
    else:
        mant, ex = np.frexp(amax / 6.0)
        byte = np.where(mant > 0.5, ex, ex - 1) + 127
    byte = np.clip(np.where(amax > 0, byte, 1), 1, 254)
    scaled = (w * np.exp2(127.0 - byte)[:, None, :]).reshape(k, n).astype(np.float32)
    by_word = np.ascontiguousarray(scaled.reshape(k // 512, 128, 4, n).transpose(0, 1, 3, 2))
    if fmt == "e4m3":
        words = by_word.astype(ml_dtypes.float8_e4m3fn).view(np.uint8)
    else:
        c = by_word.astype(ml_dtypes.float4_e2m1fn).view(np.uint8) & 0xF
        words = (c[..., 0::2] | (c[..., 1::2] << 4)).reshape(k // 512, 128, 2 * n)
    return np.ascontiguousarray(words), np.ascontiguousarray(byte.astype(np.uint8).reshape(k // 512, 16, n))


def unpack_weight(words, scales, fmt):
    g, _, n = scales.shape
    words = np.ascontiguousarray(words).reshape(g, 128, n, -1)
    if fmt == "e4m3":
        vals = words.view(ml_dtypes.float8_e4m3fn).astype(np.float64)
    else:
        nib = np.empty((g, 128, n, 4), np.uint8)
        nib[..., 0::2] = words & 0xF
        nib[..., 1::2] = words >> 4
        vals = E2M1[nib]
    vals = vals * np.repeat(np.exp2(scales.astype(np.float64) - 127.0), 8, axis=1)[..., None]
    return vals.transpose(0, 1, 3, 2).reshape(g * 512, n)


K, T, I, F, G = 512, 2048, 1024, 512, 64


def setup_inputs():
    n = np.random.standard_normal
    idx = np.random.permutation(T)[:I]
    idx2 = np.repeat(np.random.permutation(T)[:G], I // G)
    fk = mx_kscale(K)
    ptsp = pack_weight(n((K, T)) / fk[:, None], "e2m1")
    return {
        "pts_words": ptsp[0],
        "pts_scales": ptsp[1],
        "wc": (n((K, F)) * 0.7 / np.sqrt(K) * fk[:, None]).astype(np.float32),
        "wn": (n((K, F)) * 0.7 / np.sqrt(K) * fk[:, None]).astype(np.float32),
        "bias": (0.3 * n((F, 1))).astype(np.float32),
        "offs": striped(idx),
        "offs2": striped(idx2),
    }


def reference(pts_words, pts_scales, wc, wn, bias, offs, offs2):
    idx = unstriped(offs)
    idx2 = unstriped(offs2)
    ptsu = unpack_weight(pts_words, pts_scales, "e2m1")
    wcq = mxq(f64(wc), 0, "e4m3")
    ptsidx2g = ptsu[:, idx2]
    wnq = mxq(f64(wn), 0, "e4m3")
    ptsidxg = ptsu[:, idx]
    z = wcq.T @ ptsidx2g + wnq.T @ ptsidxg
    r = np.maximum(z + f64(bias), 0.0)
    y = r.reshape(F, G, I // G).max(axis=2)
    return y

@@ -1,0 +1,122 @@
+from contextlib import ExitStack
+
+import concourse.mybir as mybir
+
+F32 = mybir.dt.float32
+BF16 = mybir.dt.bfloat16
+I32 = mybir.dt.int32
+U32 = mybir.dt.uint32
+U16 = mybir.dt.uint16
+U8 = mybir.dt.uint8
+FP8X4 = mybir.dt.float8_e4m3fn_x4
+FP4X4 = mybir.dt.float4_e2m1fn_x4
+
+P = 128
+K, T, E, F, G = 512, 2048, 1024, 512, 64
+DEG = E // G
+NB = 512
+FH = 256
+FLOPS = 2 * 2 * K * F * E
+
+
+def tile_attend_edgeconv_kernel(tc, pts_words, pts_scales, wc, wn, bias, offs, offs2, out):
+    nc = tc.nc
+    with ExitStack() as ctx:
+        sb = ctx.enter_context(tc.tile_pool(name="sb", bufs=1))
+        ps = ctx.enter_context(tc.psum_pool(name="ps", bufs=1))
+
+        l_c = sb.tile([P, E // 16], U16, name="l_c")
+        l_n = sb.tile([P, E // 16], U16, name="l_n")
+        words = sb.tile([P, T], U16, name="words", align_bytes=64)
+        scales = sb.tile([P, T], U8, name="scales", align_bytes=64)
+        bias_sb = sb.tile([P, F // P], F32, name="bias_sb")
+
+        nc.vector.memset(scales[:].bitcast(I32), 0)
+        nc.sync.dma_start(l_c[:], offs2)
+        nc.sync.dma_start(words[:].bitcast(I32), pts_words[0].bitcast(I32))
+        srows = pts_scales[0].bitcast(I32).rearrange("(q r) c -> r q c", r=4)
+        for r in range(4):
+            nc.sync.dma_start(scales[r:P:32, :].bitcast(I32), srows[r])
+        nc.sync.dma_start(l_n[:], offs)
+
+        raw = {}
+        for nm, w in (("c", wc), ("n", wn)):
+            for h in range(2):
+                raw[nm, h] = sb.tile([P, 4, FH], F32, name="raw_%s%d" % (nm, h), tag="raw_%s%d" % (nm, h), align_bytes=64)
+                nc.sync.dma_start(raw[nm, h][:], w.rearrange("(p j) f -> p j f", j=4)[:, :, h * FH:(h + 1) * FH])
+        with nc.allow_non_contiguous_dma(reason="one bias value a partition"):
+            nc.sync.dma_start(bias_sb[:], bias.rearrange("(m p) o -> p (m o)", p=P))
+
+        codes = {}
+        planes = {}
+
+        def quant(nm, hs):
+            wide = FH * len(hs)
+            grp = sb.tile([P, wide, 4], BF16, name="grp_%s%d" % (nm, hs[0]), align_bytes=64)
+            for a, h in enumerate(hs):
+                nc.scalar.copy(grp[:, a * FH:(a + 1) * FH, :].rearrange("p (c i) t -> p c t i", i=4),
+                               raw[nm, h][:].rearrange("p t (c i) -> p c t i", i=4))
+            cd = sb.tile([P, wide], U32, name="codes_%s%d" % (nm, hs[0]), align_bytes=64)
+            pl = sb.tile([P, wide], U8, name="planes_%s%d" % (nm, hs[0]), align_bytes=64)
+            nc.vector.quantize_mx(out=cd[:].bitcast(FP8X4), scales=pl[:],
+                                  in_=grp[:].rearrange("p c t -> p (c t)"))
+            for a, h in enumerate(hs):
+                codes[nm, h] = cd[:, a * FH:(a + 1) * FH]
+                planes[nm, h] = pl[:, a * FH:(a + 1) * FH]
+
+        gw = {}
+        gs = {}
+
+        def gather_words(nm, lst, e, tag):
+            gw[nm, e] = sb.tile([P, NB], U16, name="gw_%s%d" % (nm, e), tag=tag, align_bytes=64)
+            nc.vector.tensor_copy(gw[nm, e][:], words[:].indirect(lst[:, e * 32:(e + 1) * 32]))
+
+        def gather_scales(nm, lst):
+            gs[nm] = sb.tile([P, E], U8, name="gs_%s" % nm, align_bytes=64)
+            nc.vector.tensor_copy(gs[nm][:], scales[:].indirect(lst[:]))
+
+        banks = {}
+
+        def mm(nm, m, e):
+            if nm == "c":
+                banks[m, e] = ps.tile([P, NB], F32, name="bank_%d%d" % (m, e))
+            h, c0 = divmod(m * P, FH)
+            nc.tensor.matmul_mx(out=banks[m, e][:],
+                                lhsT=codes[nm, h][:, c0:c0 + P].bitcast(FP8X4),
+                                lhsT_scale=planes[nm, h][:, c0:c0 + P],
+                                rhs=gw[nm, e][:].bitcast(FP4X4),
+                                rhs_scale=gs[nm][:, e * NB:(e + 1) * NB],
+                                start=(nm == "c"), stop=(nm == "n"))
+
+        best = [sb.tile([P, G], F32, name="best%d" % m) for m in range(4)]
+
+        def reduce(m, e):
+            nc.vector.tensor_reduce(out=best[m][:, e * 32:(e + 1) * 32],
+                                    in_=banks[m, e][:].rearrange("p (g j) -> p g j", j=DEG),
+                                    axis=mybir.AxisListType.X, op=mybir.AluOpType.max)
+
+        def finish(m):
+            res = sb.tile([P, G], F32, name="res%d" % m)
+            nc.scalar.activation(res[:], best[m][:], mybir.ActivationFunctionType.Relu, bias=bias_sb[:, m:m + 1])
+            nc.sync.dma_start(out[m * P:(m + 1) * P, :], res[:])
+
+        gather_words("c", l_c, 0, "gw_c0")
+        gather_words("c", l_c, 1, "gw_c1")
+        gather_scales("c", l_c)
+        gather_scales("n", l_n)
+        quant("c", (0,))
+        quant("c", (1,))
+        gather_words("n", l_n, 0, "raw_c1")
+        quant("n", (0, 1))
+        gather_words("n", l_n, 1, "raw_n1")
+        for e in (0, 1):
+            for m in range(4):
+                mm("c", m, e)
+        for e in (0, 1):
+            for m in range(4):
+                mm("n", m, e)
+        for m in range(4):
+            reduce(m, 0)
+        for m in range(4):
+            reduce(m, 1)
+            finish(m)

@@ -71,8 +71,8 @@ def tile_attend_edgeconv_kernel(tc, pts_words, pts_scales, wc, wn, bias, offs, o
             gw[nm, e] = sb.tile([P, NB], U16, name="gw_%s%d" % (nm, e), tag=tag, align_bytes=64)
             nc.vector.tensor_copy(gw[nm, e][:], words[:].indirect(lst[:, e * 32:(e + 1) * 32]))
 
-        def gather_scales(nm, lst):
-            gs[nm] = sb.tile([P, E], U8, name="gs_%s" % nm, align_bytes=64)
+        def gather_scales(nm, lst, tag):
+            gs[nm] = sb.tile([P, E], U8, name="gs_%s" % nm, tag=tag, align_bytes=64)
             nc.vector.tensor_copy(gs[nm][:], scales[:].indirect(lst[:]))
 
         banks = {}
@@ -88,35 +88,49 @@ def tile_attend_edgeconv_kernel(tc, pts_words, pts_scales, wc, wn, bias, offs, o
                                 rhs_scale=gs[nm][:, e * NB:(e + 1) * NB],
                                 start=(nm == "c"), stop=(nm == "n"))
 
+        relu = mybir.ActivationFunctionType.Relu
+
+        def group_max(dst, src):
+            nc.vector.tensor_reduce(out=dst, in_=src.rearrange("p (g j) -> p g j", j=DEG),
+                                    axis=mybir.AxisListType.X, op=mybir.AluOpType.max)
+
         best = [sb.tile([P, G], F32, name="best%d" % m) for m in range(4)]
 
         def reduce(m, e):
-            nc.vector.tensor_reduce(out=best[m][:, e * 32:(e + 1) * 32],
-                                    in_=banks[m, e][:].rearrange("p (g j) -> p g j", j=DEG),
-                                    axis=mybir.AxisListType.X, op=mybir.AluOpType.max)
+            src = banks[m, e]
+            if m == 3:
+                src = sb.tile([P, NB], F32, name="act%d" % e)
+                nc.scalar.activation(src[:], banks[m, e][:], relu, bias=bias_sb[:, m:m + 1])
+            group_max(best[m][:, e * 32:(e + 1) * 32], src[:])
 
         def finish(m):
-            res = sb.tile([P, G], F32, name="res%d" % m)
-            nc.scalar.activation(res[:], best[m][:], mybir.ActivationFunctionType.Relu, bias=bias_sb[:, m:m + 1])
+            res = best[m]
+            if m < 3:
+                res = sb.tile([P, G], F32, name="res%d" % m)
+                nc.scalar.activation(res[:], best[m][:], relu, bias=bias_sb[:, m:m + 1])
             nc.sync.dma_start(out[m * P:(m + 1) * P, :], res[:])
 
         gather_words("c", l_c, 0, "gw_c0")
         gather_words("c", l_c, 1, "gw_c1")
-        gather_scales("c", l_c)
-        gather_scales("n", l_n)
+        gather_scales("c", l_c, "gs_c")
         quant("c", (0,))
+        gather_scales("n", l_n, "raw_c0")
         quant("c", (1,))
         gather_words("n", l_n, 0, "raw_c1")
-        quant("n", (0, 1))
-        gather_words("n", l_n, 1, "raw_n1")
-        for e in (0, 1):
-            for m in range(4):
-                mm("c", m, e)
-        for e in (0, 1):
-            for m in range(4):
-                mm("n", m, e)
-        for m in range(4):
-            reduce(m, 0)
-        for m in range(4):
-            reduce(m, 1)
-            finish(m)
+        quant("n", (0,))
+        gather_words("n", l_n, 1, "raw_n0")
+        quant("n", (1,))
+        for h in (0, 1):
+            for e in (0, 1):
+                for m in (2 * h, 2 * h + 1):
+                    mm("c", m, e)
+        for h in (0, 1):
+            for e in (0, 1):
+                for m in (2 * h, 2 * h + 1):
+                    mm("n", m, e)
+        for h in (0, 1):
+            for e in (0, 1):
+                for m in (2 * h, 2 * h + 1):
+                    reduce(m, e)
+                    if e == 1:
+                        finish(m)

@@ -32,16 +32,16 @@ def tile_attend_edgeconv_kernel(tc, pts_words, pts_scales, wc, wn, bias, offs, o
         bias_sb = sb.tile([P, F // P], F32, name="bias_sb")
 
         nc.vector.memset(scales[:].bitcast(I32), 0)
-        nc.sync.dma_start(l_c[:], offs2)
         nc.sync.dma_start(words[:].bitcast(I32), pts_words[0].bitcast(I32))
+        nc.sync.dma_start(l_c[:], offs2)
+        nc.sync.dma_start(l_n[:], offs)
         srows = pts_scales[0].bitcast(I32).rearrange("(q r) c -> r q c", r=4)
         for r in range(4):
             nc.sync.dma_start(scales[r:P:32, :].bitcast(I32), srows[r])
-        nc.sync.dma_start(l_n[:], offs)
 
         raw = {}
-        for nm, w in (("c", wc), ("n", wn)):
-            for h in range(2):
+        for h in range(2):
+            for nm, w in (("c", wc), ("n", wn)):
                 raw[nm, h] = sb.tile([P, 4, FH], F32, name="raw_%s%d" % (nm, h), tag="raw_%s%d" % (nm, h), align_bytes=64)
                 nc.sync.dma_start(raw[nm, h][:], w.rearrange("(p j) f -> p j f", j=4)[:, :, h * FH:(h + 1) * FH])
         with nc.allow_non_contiguous_dma(reason="one bias value a partition"):
@@ -52,7 +52,7 @@ def tile_attend_edgeconv_kernel(tc, pts_words, pts_scales, wc, wn, bias, offs, o
 
         def quant(nm, hs):
             wide = FH * len(hs)
-            grp = sb.tile([P, wide, 4], BF16, name="grp_%s%d" % (nm, hs[0]), align_bytes=64)
+            grp = sb.tile([P, wide, 4], BF16, name="grp_%s%d" % (nm, hs[0]), tag="grp_%s%d" % (nm, hs[0]), align_bytes=64)
             for a, h in enumerate(hs):
                 nc.scalar.copy(grp[:, a * FH:(a + 1) * FH, :].rearrange("p (c i) t -> p c t i", i=4),
                                raw[nm, h][:].rearrange("p t (c i) -> p c t i", i=4))
@@ -71,9 +71,11 @@ def tile_attend_edgeconv_kernel(tc, pts_words, pts_scales, wc, wn, bias, offs, o
             gw[nm, e] = sb.tile([P, NB], U16, name="gw_%s%d" % (nm, e), tag=tag, align_bytes=64)
             nc.vector.tensor_copy(gw[nm, e][:], words[:].indirect(lst[:, e * 32:(e + 1) * 32]))
 
-        def gather_scales(nm, lst, tag):
-            gs[nm] = sb.tile([P, E], U8, name="gs_%s" % nm, tag=tag, align_bytes=64)
-            nc.vector.tensor_copy(gs[nm][:], scales[:].indirect(lst[:]))
+        def gather_scales(nm, lst, es, tag):
+            got = sb.tile([P, NB * len(es)], U8, name="gs_%s%d" % (nm, es[0]), tag=tag, align_bytes=64)
+            nc.vector.tensor_copy(got[:], scales[:].indirect(lst[:, es[0] * 32:(es[-1] + 1) * 32]))
+            for a, e in enumerate(es):
+                gs[nm, e] = got[:, a * NB:(a + 1) * NB]
 
         banks = {}
 
@@ -85,7 +87,7 @@ def tile_attend_edgeconv_kernel(tc, pts_words, pts_scales, wc, wn, bias, offs, o
                                 lhsT=codes[nm, h][:, c0:c0 + P].bitcast(FP8X4),
                                 lhsT_scale=planes[nm, h][:, c0:c0 + P],
                                 rhs=gw[nm, e][:].bitcast(FP4X4),
-                                rhs_scale=gs[nm][:, e * NB:(e + 1) * NB],
+                                rhs_scale=gs[nm, e],
                                 start=(nm == "c"), stop=(nm == "n"))
 
         relu = mybir.ActivationFunctionType.Relu
@@ -94,7 +96,7 @@ def tile_attend_edgeconv_kernel(tc, pts_words, pts_scales, wc, wn, bias, offs, o
             nc.vector.tensor_reduce(out=dst, in_=src.rearrange("p (g j) -> p g j", j=DEG),
                                     axis=mybir.AxisListType.X, op=mybir.AluOpType.max)
 
-        best = [sb.tile([P, G], F32, name="best%d" % m) for m in range(4)]
+        best = {}
 
         def reduce(m, e):
             src = banks[m, e]
@@ -106,28 +108,39 @@ def tile_attend_edgeconv_kernel(tc, pts_words, pts_scales, wc, wn, bias, offs, o
         def finish(m):
             res = best[m]
             if m < 3:
-                res = sb.tile([P, G], F32, name="res%d" % m)
-                nc.scalar.activation(res[:], best[m][:], relu, bias=bias_sb[:, m:m + 1])
-            nc.sync.dma_start(out[m * P:(m + 1) * P, :], res[:])
+                act = sb.tile([P, G], F32, name="res%d" % m)
+                res = act[:]
+                nc.scalar.activation(res, best[m], relu, bias=bias_sb[:, m:m + 1])
+            nc.sync.dma_start(out[m * P:(m + 1) * P, :], res)
 
         gather_words("c", l_c, 0, "gw_c0")
         gather_words("c", l_c, 1, "gw_c1")
-        gather_scales("c", l_c, "gs_c")
+        gather_words("n", l_n, 0, "gw_n0")
+        gather_scales("c", l_c, (0, 1), "gs_c")
         quant("c", (0,))
-        gather_scales("n", l_n, "raw_c0")
-        quant("c", (1,))
-        gather_words("n", l_n, 0, "raw_c1")
+        gather_scales("n", l_n, (0,), "raw_c0")
         quant("n", (0,))
-        gather_words("n", l_n, 1, "raw_n0")
+        gather_scales("n", l_n, (1,), "raw_n0")
+        quant("c", (1,))
+        gather_words("n", l_n, 1, "raw_c1")
         quant("n", (1,))
-        for h in (0, 1):
-            for e in (0, 1):
-                for m in (2 * h, 2 * h + 1):
-                    mm("c", m, e)
-        for h in (0, 1):
-            for e in (0, 1):
-                for m in (2 * h, 2 * h + 1):
-                    mm("n", m, e)
+        for h, tag in ((0, "grp_c1"), (1, "best1")):
+            pair = sb.tile([P, 2 * G], F32, name="best%d" % h, tag=tag, align_bytes=64)
+            best[2 * h] = pair[:, 0:G]
+            best[2 * h + 1] = pair[:, G:2 * G]
+        for e in (0, 1):
+            for m in (0, 1):
+                mm("c", m, e)
+        for m in (0, 1):
+            mm("n", m, 0)
+        for e in (0, 1):
+            for m in (2, 3):
+                mm("c", m, e)
+        for m in (0, 1):
+            mm("n", m, 1)
+        for e in (0, 1):
+            for m in (2, 3):
+                mm("n", m, e)
         for h in (0, 1):
             for e in (0, 1):
                 for m in (2 * h, 2 * h + 1):

@@ -27,12 +27,13 @@ def tile_attend_edgeconv_kernel(tc, pts_words, pts_scales, wc, wn, bias, offs, o
 
         l_c = sb.tile([P, E // 16], U16, name="l_c")
         l_n = sb.tile([P, E // 16], U16, name="l_n")
-        words = sb.tile([P, T], U16, name="words", align_bytes=64)
+        words = sb.tile([P, 2 * T], U16, name="words", align_bytes=64)
         scales = sb.tile([P, T], U8, name="scales", align_bytes=64)
         bias_sb = sb.tile([P, F // P], F32, name="bias_sb")
 
         nc.vector.memset(scales[:].bitcast(I32), 0)
-        nc.sync.dma_start(words[:].bitcast(I32), pts_words[0].bitcast(I32))
+        nc.vector.memset(words[:, T:].bitcast(I32), 0)
+        nc.sync.dma_start(words[:, :T].bitcast(I32), pts_words[0].bitcast(I32))
         nc.sync.dma_start(l_c[:], offs2)
         nc.sync.dma_start(l_n[:], offs)
         srows = pts_scales[0].bitcast(I32).rearrange("(q r) c -> r q c", r=4)
@@ -64,18 +65,20 @@ def tile_attend_edgeconv_kernel(tc, pts_words, pts_scales, wc, wn, bias, offs, o
                 codes[nm, h] = cd[:, a * FH:(a + 1) * FH]
                 planes[nm, h] = pl[:, a * FH:(a + 1) * FH]
 
-        gw = {}
-        gs = {}
+        def gather(name, dtype, window, lst, first, count, tag):
+            got = sb.tile([P, count], dtype, name=name, tag=tag, align_bytes=64)
+            nc.vector.tensor_copy(got[:], window[:].indirect(lst[:, first // 16:(first + count) // 16]))
+            return [got[:, c:c + NB] for c in range(0, count, NB)]
 
-        def gather_words(nm, lst, e, tag):
-            gw[nm, e] = sb.tile([P, NB], U16, name="gw_%s%d" % (nm, e), tag=tag, align_bytes=64)
-            nc.vector.tensor_copy(gw[nm, e][:], words[:].indirect(lst[:, e * 32:(e + 1) * 32]))
-
-        def gather_scales(nm, lst, es, tag):
-            got = sb.tile([P, NB * len(es)], U8, name="gs_%s%d" % (nm, es[0]), tag=tag, align_bytes=64)
-            nc.vector.tensor_copy(got[:], scales[:].indirect(lst[:, es[0] * 32:(es[-1] + 1) * 32]))
-            for a, e in enumerate(es):
-                gs[nm, e] = got[:, a * NB:(a + 1) * NB]
+        gw = {"c": gather("gw_c", U16, words, l_c, 0, E, "gw_c"),
+              "n": gather("gw_n0", U16, words, l_n, 0, NB, "gw_n0")}
+        gs = {"c": gather("gs_c", U8, scales, l_c, 0, E, "gs_c")}
+        quant("c", (0,))
+        gs["n"] = gather("gs_n", U8, scales, l_n, 0, E, "raw_c0")
+        quant("n", (0,))
+        quant("c", (1,))
+        gw["n"] = gw["n"] + gather("gw_n1", U16, words, l_n, NB, NB, "raw_c1")
+        quant("n", (1,))
 
         banks = {}
 
@@ -86,64 +89,48 @@ def tile_attend_edgeconv_kernel(tc, pts_words, pts_scales, wc, wn, bias, offs, o
             nc.tensor.matmul_mx(out=banks[m, e][:],
                                 lhsT=codes[nm, h][:, c0:c0 + P].bitcast(FP8X4),
                                 lhsT_scale=planes[nm, h][:, c0:c0 + P],
-                                rhs=gw[nm, e][:].bitcast(FP4X4),
-                                rhs_scale=gs[nm, e],
+                                rhs=gw[nm][e].bitcast(FP4X4),
+                                rhs_scale=gs[nm][e],
                                 start=(nm == "c"), stop=(nm == "n"))
 
-        relu = mybir.ActivationFunctionType.Relu
+        for nm, m, e in (("c", 0, 0), ("c", 1, 0), ("c", 0, 1), ("c", 1, 1), ("n", 0, 0), ("n", 1, 0),
+                         ("c", 2, 0), ("c", 3, 0), ("n", 0, 1), ("n", 1, 1), ("n", 2, 0), ("n", 3, 0),
+                         ("c", 2, 1), ("n", 2, 1), ("c", 3, 1), ("n", 3, 1)):
+            mm(nm, m, e)
 
-        def group_max(dst, src):
-            nc.vector.tensor_reduce(out=dst, in_=src.rearrange("p (g j) -> p g j", j=DEG),
+        relu = mybir.ActivationFunctionType.Relu
+        HALF = NB // 2
+
+        def group_max(dst, src, width):
+            nc.vector.tensor_reduce(out=dst, in_=src.rearrange("p (g j) -> p g j", j=width),
                                     axis=mybir.AxisListType.X, op=mybir.AluOpType.max)
 
+        pairs = sb.tile([P, NB], F32, name="pairs")
+        lows, steps = [], []
+        for e in (0, 1):
+            act = sb.tile([P, 2, HALF], F32, name="act%d" % e)
+            nc.scalar.activation(act[:].rearrange("p h (g j) -> p h g j", j=DEG // 2),
+                                 banks[0, e][:].rearrange("p (g h j) -> p h g j", h=2, j=DEG // 2),
+                                 relu, bias=bias_sb[:, 0:1])
+            diff = sb.tile([P, HALF], F32, name="diff%d" % e, tag=("grp_n1", "diff1")[e], align_bytes=64)
+            nc.gpsimd.tensor_tensor(diff[:], act[:, 1, :], act[:, 0, :], mybir.AluOpType.subtract)
+            step = sb.tile([P, HALF], F32, name="step%d" % e)
+            nc.scalar.activation(step[:], diff[:], relu)
+            lows.append(act[:, 0, :])
+            steps.append(step)
+        for e in (0, 1):
+            nc.gpsimd.tensor_tensor(pairs[:, e * HALF:(e + 1) * HALF], lows[e], steps[e][:], mybir.AluOpType.add)
+
         best = {}
-
-        def reduce(m, e):
-            src = banks[m, e]
-            if m == 3:
-                src = sb.tile([P, NB], F32, name="act%d" % e)
-                nc.scalar.activation(src[:], banks[m, e][:], relu, bias=bias_sb[:, m:m + 1])
-            group_max(best[m][:, e * 32:(e + 1) * 32], src[:])
-
-        def finish(m):
-            res = best[m]
-            if m < 3:
-                act = sb.tile([P, G], F32, name="res%d" % m)
-                res = act[:]
-                nc.scalar.activation(res, best[m], relu, bias=bias_sb[:, m:m + 1])
-            nc.sync.dma_start(out[m * P:(m + 1) * P, :], res)
-
-        gather_words("c", l_c, 0, "gw_c0")
-        gather_words("c", l_c, 1, "gw_c1")
-        gather_words("n", l_n, 0, "gw_n0")
-        gather_scales("c", l_c, (0, 1), "gs_c")
-        quant("c", (0,))
-        gather_scales("n", l_n, (0,), "raw_c0")
-        quant("n", (0,))
-        gather_scales("n", l_n, (1,), "raw_n0")
-        quant("c", (1,))
-        gather_words("n", l_n, 1, "raw_c1")
-        quant("n", (1,))
-        for h, tag in ((0, "grp_c1"), (1, "best1")):
-            pair = sb.tile([P, 2 * G], F32, name="best%d" % h, tag=tag, align_bytes=64)
-            best[2 * h] = pair[:, 0:G]
-            best[2 * h + 1] = pair[:, G:2 * G]
+        for m in (1, 2, 3):
+            best[m] = sb.tile([P, G], F32, name="best%d" % m)
+        for m, e in ((1, 0), (1, 1), (2, 0), (3, 0), (2, 1), (3, 1)):
+            group_max(best[m][:, e * 32:(e + 1) * 32], banks[m, e][:], DEG)
+            if e == 1:
+                res = sb.tile([P, G], F32, name="res%d" % m)
+                nc.scalar.activation(res[:], best[m][:], relu, bias=bias_sb[:, m:m + 1])
+                nc.sync.dma_start(out[m * P:(m + 1) * P, :], res[:])
+        last = sb.tile([P, G], F32, name="last")
         for e in (0, 1):
-            for m in (0, 1):
-                mm("c", m, e)
-        for m in (0, 1):
-            mm("n", m, 0)
-        for e in (0, 1):
-            for m in (2, 3):
-                mm("c", m, e)
-        for m in (0, 1):
-            mm("n", m, 1)
-        for e in (0, 1):
-            for m in (2, 3):
-                mm("n", m, e)
-        for h in (0, 1):
-            for e in (0, 1):
-                for m in (2 * h, 2 * h + 1):
-                    reduce(m, e)
-                    if e == 1:
-                        finish(m)
+            group_max(last[:, e * 32:(e + 1) * 32], pairs[:, e * HALF:(e + 1) * HALF], DEG // 2)
+        nc.sync.dma_start(out[0:P, :], last[:])

@@ -27,7 +27,7 @@ def tile_attend_edgeconv_kernel(tc, pts_words, pts_scales, wc, wn, bias, offs, o
 
         l_c = sb.tile([P, E // 16], U16, name="l_c")
         l_n = sb.tile([P, E // 16], U16, name="l_n")
-        words = sb.tile([P, 2 * T], U16, name="words", align_bytes=64)
+        words = sb.tile([P, 2 * T], U16, name="words", tag="words", align_bytes=64)
         scales = sb.tile([P, T], U8, name="scales", align_bytes=64)
         bias_sb = sb.tile([P, F // P], F32, name="bias_sb")
 
@@ -74,8 +74,9 @@ def tile_attend_edgeconv_kernel(tc, pts_words, pts_scales, wc, wn, bias, offs, o
               "n": gather("gw_n0", U16, words, l_n, 0, NB, "gw_n0")}
         gs = {"c": gather("gs_c", U8, scales, l_c, 0, E, "gs_c")}
         quant("c", (0,))
-        gs["n"] = gather("gs_n", U8, scales, l_n, 0, E, "raw_c0")
+        gs["n"] = gather("gs_n0", U8, scales, l_n, 0, NB, "raw_c0")
         quant("n", (0,))
+        gs["n"] = gs["n"] + gather("gs_n1", U8, scales, l_n, NB, NB, "raw_n0")
         quant("c", (1,))
         gw["n"] = gw["n"] + gather("gw_n1", U16, words, l_n, NB, NB, "raw_c1")
         quant("n", (1,))
@@ -94,7 +95,7 @@ def tile_attend_edgeconv_kernel(tc, pts_words, pts_scales, wc, wn, bias, offs, o
                                 start=(nm == "c"), stop=(nm == "n"))
 
         for nm, m, e in (("c", 0, 0), ("c", 1, 0), ("c", 0, 1), ("c", 1, 1), ("n", 0, 0), ("n", 1, 0),
-                         ("c", 2, 0), ("c", 3, 0), ("n", 0, 1), ("n", 1, 1), ("n", 2, 0), ("n", 3, 0),
+                         ("c", 2, 0), ("c", 3, 0), ("n", 1, 1), ("n", 0, 1), ("n", 2, 0), ("n", 3, 0),
                          ("c", 2, 1), ("n", 2, 1), ("c", 3, 1), ("n", 3, 1)):
             mm(nm, m, e)
 
@@ -105,32 +106,39 @@ def tile_attend_edgeconv_kernel(tc, pts_words, pts_scales, wc, wn, bias, offs, o
             nc.vector.tensor_reduce(out=dst, in_=src.rearrange("p (g j) -> p g j", j=width),
                                     axis=mybir.AxisListType.X, op=mybir.AluOpType.max)
 
-        pairs = sb.tile([P, NB], F32, name="pairs")
-        lows, steps = [], []
+        shares = (32, 24)
+        pairs = sb.tile([P, 8 * sum(shares)], F32, name="pairs")
+        acts, steps = [], []
         for e in (0, 1):
-            act = sb.tile([P, 2, HALF], F32, name="act%d" % e)
+            act = sb.tile([P, 2, 8 * shares[e]], F32, name="act%d" % e)
             nc.scalar.activation(act[:].rearrange("p h (g j) -> p h g j", j=DEG // 2),
-                                 banks[0, e][:].rearrange("p (g h j) -> p h g j", h=2, j=DEG // 2),
+                                 banks[0, e][:, :DEG * shares[e]].rearrange("p (g h j) -> p h g j", h=2, j=DEG // 2),
                                  relu, bias=bias_sb[:, 0:1])
-            diff = sb.tile([P, HALF], F32, name="diff%d" % e, tag=("grp_n1", "diff1")[e], align_bytes=64)
+            acts.append(act)
+        for e, act in enumerate(acts):
+            diff = sb.tile([P, 8 * shares[e]], F32, name="diff%d" % e, tag=("words", "diff1")[e], align_bytes=64)
             nc.gpsimd.tensor_tensor(diff[:], act[:, 1, :], act[:, 0, :], mybir.AluOpType.subtract)
-            step = sb.tile([P, HALF], F32, name="step%d" % e)
+            step = sb.tile([P, 8 * shares[e]], F32, name="step%d" % e)
             nc.scalar.activation(step[:], diff[:], relu)
-            lows.append(act[:, 0, :])
             steps.append(step)
+        cuts = (0, 8 * shares[0], 8 * sum(shares))
         for e in (0, 1):
-            nc.gpsimd.tensor_tensor(pairs[:, e * HALF:(e + 1) * HALF], lows[e], steps[e][:], mybir.AluOpType.add)
+            nc.gpsimd.tensor_tensor(pairs[:, cuts[e]:cuts[e + 1]], acts[e][:, 0, :], steps[e][:], mybir.AluOpType.add)
 
         best = {}
         for m in (1, 2, 3):
-            best[m] = sb.tile([P, G], F32, name="best%d" % m)
+            best[m] = sb.tile([P, G], F32, name="best%d" % m, tag="raw_n1" if m == 1 else "best%d" % m, align_bytes=64)
+        last = sb.tile([P, G], F32, name="last")
+        rest = sb.tile([P, G - sum(shares)], F32, name="rest")
         for m, e in ((1, 0), (1, 1), (2, 0), (3, 0), (2, 1), (3, 1)):
             group_max(best[m][:, e * 32:(e + 1) * 32], banks[m, e][:], DEG)
             if e == 1:
                 res = sb.tile([P, G], F32, name="res%d" % m)
                 nc.scalar.activation(res[:], best[m][:], relu, bias=bias_sb[:, m:m + 1])
                 nc.sync.dma_start(out[m * P:(m + 1) * P, :], res[:])
-        last = sb.tile([P, G], F32, name="last")
+            if (m, e) == (1, 1):
+                group_max(rest[:], banks[0, 1][:, DEG * shares[1]:], DEG)
+                nc.scalar.activation(last[:, sum(shares):], rest[:], relu, bias=bias_sb[:, 0:1])
         for e in (0, 1):
-            group_max(last[:, e * 32:(e + 1) * 32], pairs[:, e * HALF:(e + 1) * HALF], DEG // 2)
+            group_max(last[:, cuts[e] // 8:cuts[e + 1] // 8], pairs[:, cuts[e]:cuts[e + 1]], DEG // 2)
         nc.sync.dma_start(out[0:P, :], last[:])

@@ -15,7 +15,7 @@ P = 128
 K, T, E, F, G = 512, 2048, 1024, 512, 64
 DEG = E // G
 NB = 512
-FH = 256
+GH = NB // DEG
 FLOPS = 2 * 2 * K * F * E
 
 
@@ -40,30 +40,36 @@ def tile_attend_edgeconv_kernel(tc, pts_words, pts_scales, wc, wn, bias, offs, o
         for r in range(4):
             nc.sync.dma_start(scales[r:P:32, :].bitcast(I32), srows[r])
 
+        chunks = (("c", 0, 2), ("n", 0, 2), ("c", 2, 2), ("n", 2, 1), ("n", 3, 1))
         raw = {}
-        for h in range(2):
-            for nm, w in (("c", wc), ("n", wn)):
-                raw[nm, h] = sb.tile([P, 4, FH], F32, name="raw_%s%d" % (nm, h), tag="raw_%s%d" % (nm, h), align_bytes=64)
-                nc.sync.dma_start(raw[nm, h][:], w.rearrange("(p j) f -> p j f", j=4)[:, :, h * FH:(h + 1) * FH])
+        for nm, m0, mt in chunks:
+            w = wc if nm == "c" else wn
+            raw[nm, m0] = sb.tile([P, 4, mt * P], F32, name="raw_%s%d" % (nm, m0), tag="raw_%s%d" % (nm, m0), align_bytes=64)
+            nc.sync.dma_start(raw[nm, m0][:], w.rearrange("(p j) f -> p j f", j=4)[:, :, m0 * P:(m0 + mt) * P])
         with nc.allow_non_contiguous_dma(reason="one bias value a partition"):
             nc.sync.dma_start(bias_sb[:], bias.rearrange("(m p) o -> p (m o)", p=P))
 
         codes = {}
         planes = {}
 
-        def quant(nm, hs):
-            wide = FH * len(hs)
-            grp = sb.tile([P, wide, 4], BF16, name="grp_%s%d" % (nm, hs[0]), tag="grp_%s%d" % (nm, hs[0]), align_bytes=64)
-            for a, h in enumerate(hs):
-                nc.scalar.copy(grp[:, a * FH:(a + 1) * FH, :].rearrange("p (c i) t -> p c t i", i=4),
-                               raw[nm, h][:].rearrange("p t (c i) -> p c t i", i=4))
-            cd = sb.tile([P, wide], U32, name="codes_%s%d" % (nm, hs[0]), align_bytes=64)
-            pl = sb.tile([P, wide], U8, name="planes_%s%d" % (nm, hs[0]), align_bytes=64)
+        def quant(tiles):
+            name = "%s%d" % tiles[0]
+            grp = sb.tile([P, 2 * P, 4], BF16, name="grp_" + name, tag="grp_" + name, align_bytes=64)
+            if tiles[0][0] == tiles[1][0]:
+                nc.scalar.copy(grp[:].rearrange("p (c i) t -> p c t i", i=4),
+                               raw[tiles[0]][:].rearrange("p t (c i) -> p c t i", i=4))
+            else:
+                for a, (nm, m) in enumerate(tiles):
+                    src = raw[nm, 2][:, :, (m - 2) * P:(m - 1) * P] if nm == "c" else raw[nm, m][:]
+                    nc.scalar.copy(grp[:, a * P:(a + 1) * P, :].rearrange("p (c i) t -> p c t i", i=4),
+                                   src.rearrange("p t (c i) -> p c t i", i=4))
+            cd = sb.tile([P, 2 * P], U32, name="codes_" + name, align_bytes=64)
+            pl = sb.tile([P, 2 * P], U8, name="planes_" + name, align_bytes=64)
             nc.vector.quantize_mx(out=cd[:].bitcast(FP8X4), scales=pl[:],
                                   in_=grp[:].rearrange("p c t -> p (c t)"))
-            for a, h in enumerate(hs):
-                codes[nm, h] = cd[:, a * FH:(a + 1) * FH]
-                planes[nm, h] = pl[:, a * FH:(a + 1) * FH]
+            for a, key in enumerate(tiles):
+                codes[key] = cd[:, a * P:(a + 1) * P]
+                planes[key] = pl[:, a * P:(a + 1) * P]
 
         def gather(name, dtype, window, lst, first, count, tag):
             got = sb.tile([P, count], dtype, name=name, tag=tag, align_bytes=64)
@@ -73,30 +79,30 @@ def tile_attend_edgeconv_kernel(tc, pts_words, pts_scales, wc, wn, bias, offs, o
         gw = {"c": gather("gw_c", U16, words, l_c, 0, E, "gw_c"),
               "n": gather("gw_n0", U16, words, l_n, 0, NB, "gw_n0")}
         gs = {"c": gather("gs_c", U8, scales, l_c, 0, E, "gs_c")}
-        quant("c", (0,))
+        quant((("c", 0), ("c", 1)))
         gs["n"] = gather("gs_n0", U8, scales, l_n, 0, NB, "raw_c0")
-        quant("n", (0,))
+        quant((("n", 0), ("n", 1)))
         gs["n"] = gs["n"] + gather("gs_n1", U8, scales, l_n, NB, NB, "raw_n0")
-        quant("c", (1,))
-        gw["n"] = gw["n"] + gather("gw_n1", U16, words, l_n, NB, NB, "raw_c1")
-        quant("n", (1,))
+        quant((("c", 2), ("n", 2)))
+        gw["n"] = gw["n"] + gather("gw_n1", U16, words, l_n, NB, NB, "raw_n2")
+        quant((("c", 3), ("n", 3)))
 
         banks = {}
+        reuse = {(1, 1): (2, 0)}
 
         def mm(nm, m, e):
             if nm == "c":
-                banks[m, e] = ps.tile([P, NB], F32, name="bank_%d%d" % (m, e))
-            h, c0 = divmod(m * P, FH)
+                banks[m, e] = ps.tile([P, NB], F32, name="bank_%d%d" % (m, e), tag="bank_%d%d" % reuse.get((m, e), (m, e)))
             nc.tensor.matmul_mx(out=banks[m, e][:],
-                                lhsT=codes[nm, h][:, c0:c0 + P].bitcast(FP8X4),
-                                lhsT_scale=planes[nm, h][:, c0:c0 + P],
+                                lhsT=codes[nm, m].bitcast(FP8X4),
+                                lhsT_scale=planes[nm, m],
                                 rhs=gw[nm][e].bitcast(FP4X4),
                                 rhs_scale=gs[nm][e],
                                 start=(nm == "c"), stop=(nm == "n"))
 
-        for nm, m, e in (("c", 0, 0), ("c", 1, 0), ("c", 0, 1), ("c", 1, 1), ("n", 0, 0), ("n", 1, 0),
-                         ("c", 2, 0), ("c", 3, 0), ("n", 1, 1), ("n", 0, 1), ("n", 2, 0), ("n", 3, 0),
-                         ("c", 2, 1), ("n", 2, 1), ("c", 3, 1), ("n", 3, 1)):
+        for nm, m, e in (("c", 0, 0), ("c", 1, 0), ("c", 0, 1), ("n", 0, 0), ("n", 1, 0),
+                         ("c", 2, 0), ("n", 2, 0), ("c", 2, 1), ("n", 0, 1), ("n", 2, 1),
+                         ("c", 3, 0), ("n", 3, 0), ("c", 3, 1), ("n", 3, 1)):
             mm(nm, m, e)
 
         relu = mybir.ActivationFunctionType.Relu
@@ -106,39 +112,37 @@ def tile_attend_edgeconv_kernel(tc, pts_words, pts_scales, wc, wn, bias, offs, o
             nc.vector.tensor_reduce(out=dst, in_=src.rearrange("p (g j) -> p g j", j=width),
                                     axis=mybir.AxisListType.X, op=mybir.AluOpType.max)
 
-        shares = (32, 24)
-        pairs = sb.tile([P, 8 * sum(shares)], F32, name="pairs")
-        acts, steps = [], []
-        for e in (0, 1):
-            act = sb.tile([P, 2, 8 * shares[e]], F32, name="act%d" % e)
+        acts, steps, pairs = [], [], []
+        for m in (0, 1):
+            act = sb.tile([P, 2, HALF], F32, name="act%d" % m)
             nc.scalar.activation(act[:].rearrange("p h (g j) -> p h g j", j=DEG // 2),
-                                 banks[0, e][:, :DEG * shares[e]].rearrange("p (g h j) -> p h g j", h=2, j=DEG // 2),
-                                 relu, bias=bias_sb[:, 0:1])
+                                 banks[m, 0][:].rearrange("p (g h j) -> p h g j", h=2, j=DEG // 2),
+                                 relu, bias=bias_sb[:, m:m + 1])
             acts.append(act)
-        for e, act in enumerate(acts):
-            diff = sb.tile([P, 8 * shares[e]], F32, name="diff%d" % e, tag=("words", "diff1")[e], align_bytes=64)
+        for m, act in enumerate(acts):
+            diff = sb.tile([P, HALF], F32, name="diff%d" % m, tag=("words", "diff1")[m], align_bytes=64)
             nc.gpsimd.tensor_tensor(diff[:], act[:, 1, :], act[:, 0, :], mybir.AluOpType.subtract)
-            step = sb.tile([P, 8 * shares[e]], F32, name="step%d" % e)
+            step = sb.tile([P, HALF], F32, name="step%d" % m)
             nc.scalar.activation(step[:], diff[:], relu)
             steps.append(step)
-        cuts = (0, 8 * shares[0], 8 * sum(shares))
-        for e in (0, 1):
-            nc.gpsimd.tensor_tensor(pairs[:, cuts[e]:cuts[e + 1]], acts[e][:, 0, :], steps[e][:], mybir.AluOpType.add)
+        for m in (0, 1):
+            pair = sb.tile([P, HALF], F32, name="pair%d" % m)
+            nc.gpsimd.tensor_tensor(pair[:], acts[m][:, 0, :], steps[m][:], mybir.AluOpType.add)
+            pairs.append(pair)
 
-        best = {}
-        for m in (1, 2, 3):
-            best[m] = sb.tile([P, G], F32, name="best%d" % m, tag="raw_n1" if m == 1 else "best%d" % m, align_bytes=64)
-        last = sb.tile([P, G], F32, name="last")
-        rest = sb.tile([P, G - sum(shares)], F32, name="rest")
-        for m, e in ((1, 0), (1, 1), (2, 0), (3, 0), (2, 1), (3, 1)):
-            group_max(best[m][:, e * 32:(e + 1) * 32], banks[m, e][:], DEG)
+        best = sb.tile([P, 4 * G], F32, name="best", tag="raw_n3", align_bytes=64)
+        res = sb.tile([P, 4 * G], F32, name="res", tag="diff1", align_bytes=64)
+        for m, e in ((2, 0), (0, 1), (2, 1), (3, 0), (3, 1), (1, 1)):
+            if (m, e) in reuse:
+                mm("c", m, e)
+                mm("n", m, e)
+            group_max(best[:, m * G + e * GH:m * G + (e + 1) * GH], banks[m, e][:], DEG)
             if e == 1:
-                res = sb.tile([P, G], F32, name="res%d" % m)
-                nc.scalar.activation(res[:], best[m][:], relu, bias=bias_sb[:, m:m + 1])
-                nc.sync.dma_start(out[m * P:(m + 1) * P, :], res[:])
-            if (m, e) == (1, 1):
-                group_max(rest[:], banks[0, 1][:, DEG * shares[1]:], DEG)
-                nc.scalar.activation(last[:, sum(shares):], rest[:], relu, bias=bias_sb[:, 0:1])
-        for e in (0, 1):
-            group_max(last[:, cuts[e] // 8:cuts[e + 1] // 8], pairs[:, cuts[e]:cuts[e + 1]], DEG // 2)
-        nc.sync.dma_start(out[0:P, :], last[:])
+                first = m * G + (GH if m < 2 else 0)
+                nc.scalar.activation(res[:, first:(m + 1) * G], best[:, first:(m + 1) * G], relu, bias=bias_sb[:, m:m + 1])
+            if (m, e) == (3, 1):
+                nc.sync.dma_start(out[2 * P:, :].rearrange("(m p) g -> p m g", p=P),
+                                  res[:, 2 * G:].rearrange("p (m g) -> p m g", g=G))
+        for m in (0, 1):
+            group_max(res[:, m * G:m * G + GH], pairs[m][:], DEG // 2)
+            nc.sync.dma_start(out[m * P:(m + 1) * P, :], res[:, m * G:(m + 1) * G])

@@ -33,8 +33,8 @@ def tile_attend_edgeconv_kernel(tc, pts_words, pts_scales, wc, wn, bias, offs, o
 
         nc.vector.memset(scales[:].bitcast(I32), 0)
         nc.vector.memset(words[:, T:].bitcast(I32), 0)
-        nc.sync.dma_start(words[:, :T].bitcast(I32), pts_words[0].bitcast(I32))
         nc.sync.dma_start(l_c[:], offs2)
+        nc.sync.dma_start(words[:, :T].bitcast(I32), pts_words[0].bitcast(I32))
         nc.sync.dma_start(l_n[:], offs)
         srows = pts_scales[0].bitcast(I32).rearrange("(q r) c -> r q c", r=4)
         for r in range(4):

@@ -23,6 +23,7 @@ def tile_attend_edgeconv_kernel(tc, pts_words, pts_scales, wc, wn, bias, offs, o
     nc = tc.nc
     with ExitStack() as ctx:
         sb = ctx.enter_context(tc.tile_pool(name="sb", bufs=1))
+        late = ctx.enter_context(tc.tile_pool(name="late", bufs=1))
         ps = ctx.enter_context(tc.psum_pool(name="ps", bufs=1))
 
         l_c = sb.tile([P, E // 16], U16, name="l_c")
@@ -31,61 +32,66 @@ def tile_attend_edgeconv_kernel(tc, pts_words, pts_scales, wc, wn, bias, offs, o
         scales = sb.tile([P, T], U8, name="scales", align_bytes=64)
         bias_sb = sb.tile([P, F // P], F32, name="bias_sb")
 
+        raw = {}
+
+        def load(nm, m0, mt):
+            w = wc if nm == "c" else wn
+            if m0 >= 2:
+                tile = late.tile([P, 4, mt * P], F32, name="raw_%s%d" % (nm, m0), align_bytes=64, offset=(m0 - 2) * 8 * NB)
+            else:
+                tile = sb.tile([P, 4, mt * P], F32, name="raw_%s%d" % (nm, m0), tag="raw_%s%d" % (nm, m0), align_bytes=64)
+            nc.sync.dma_start(tile[:], w.rearrange("(p j) f -> p j f", j=4)[:, :, m0 * P:(m0 + mt) * P])
+            for a in range(mt):
+                raw[nm, m0 + a] = tile[:, :, a * P:(a + 1) * P]
+
         nc.vector.memset(scales[:].bitcast(I32), 0)
         nc.vector.memset(words[:, T:].bitcast(I32), 0)
+        load("c", 0, 1)
         nc.sync.dma_start(l_c[:], offs2)
-        nc.sync.dma_start(words[:, :T].bitcast(I32), pts_words[0].bitcast(I32))
-        nc.sync.dma_start(l_n[:], offs)
         srows = pts_scales[0].bitcast(I32).rearrange("(q r) c -> r q c", r=4)
         for r in range(4):
             nc.sync.dma_start(scales[r:P:32, :].bitcast(I32), srows[r])
-
-        chunks = (("c", 0, 2), ("n", 0, 2), ("c", 2, 2), ("n", 2, 1), ("n", 3, 1))
-        raw = {}
-        for nm, m0, mt in chunks:
-            w = wc if nm == "c" else wn
-            raw[nm, m0] = sb.tile([P, 4, mt * P], F32, name="raw_%s%d" % (nm, m0), tag="raw_%s%d" % (nm, m0), align_bytes=64)
-            nc.sync.dma_start(raw[nm, m0][:], w.rearrange("(p j) f -> p j f", j=4)[:, :, m0 * P:(m0 + mt) * P])
+        nc.sync.dma_start(l_n[:], offs)
+        nc.sync.dma_start(words[:, :T].bitcast(I32), pts_words[0].bitcast(I32))
+        for nm, m0, mt in (("n", 0, 2), ("c", 1, 2), ("n", 2, 2), ("c", 3, 1)):
+            load(nm, m0, mt)
         with nc.allow_non_contiguous_dma(reason="one bias value a partition"):
             nc.sync.dma_start(bias_sb[:], bias.rearrange("(m p) o -> p (m o)", p=P))
 
         codes = {}
         planes = {}
 
-        def quant(tiles):
-            name = "%s%d" % tiles[0]
-            grp = sb.tile([P, 2 * P, 4], BF16, name="grp_" + name, tag="grp_" + name, align_bytes=64)
-            if tiles[0][0] == tiles[1][0]:
-                nc.scalar.copy(grp[:].rearrange("p (c i) t -> p c t i", i=4),
-                               raw[tiles[0]][:].rearrange("p t (c i) -> p c t i", i=4))
-            else:
-                for a, (nm, m) in enumerate(tiles):
-                    src = raw[nm, 2][:, :, (m - 2) * P:(m - 1) * P] if nm == "c" else raw[nm, m][:]
-                    nc.scalar.copy(grp[:, a * P:(a + 1) * P, :].rearrange("p (c i) t -> p c t i", i=4),
-                                   src.rearrange("p t (c i) -> p c t i", i=4))
-            cd = sb.tile([P, 2 * P], U32, name="codes_" + name, align_bytes=64)
-            pl = sb.tile([P, 2 * P], U8, name="planes_" + name, align_bytes=64)
+        def quant(m):
+            grp = sb.tile([P, 2 * P, 4], BF16, name="grp%d" % m, align_bytes=64)
+            for a, nm in enumerate("cn"):
+                nc.scalar.copy(grp[:, a * P:(a + 1) * P, :].rearrange("p (c i) t -> p c t i", i=4),
+                               raw[nm, m].rearrange("p t (c i) -> p c t i", i=4))
+            cd = sb.tile([P, 2 * P], U32, name="codes%d" % m, align_bytes=64)
+            pl = sb.tile([P, 2 * P], U8, name="planes%d" % m, align_bytes=64)
             nc.vector.quantize_mx(out=cd[:].bitcast(FP8X4), scales=pl[:],
                                   in_=grp[:].rearrange("p c t -> p (c t)"))
-            for a, key in enumerate(tiles):
-                codes[key] = cd[:, a * P:(a + 1) * P]
-                planes[key] = pl[:, a * P:(a + 1) * P]
+            for a, nm in enumerate("cn"):
+                codes[nm, m] = cd[:, a * P:(a + 1) * P]
+                planes[nm, m] = pl[:, a * P:(a + 1) * P]
 
         def gather(name, dtype, window, lst, first, count, tag):
-            got = sb.tile([P, count], dtype, name=name, tag=tag, align_bytes=64)
+            if tag is None:
+                got = late.tile([P, count], dtype, name=name, align_bytes=64, offset=0)
+            else:
+                got = sb.tile([P, count], dtype, name=name, tag=tag, align_bytes=64)
             nc.vector.tensor_copy(got[:], window[:].indirect(lst[:, first // 16:(first + count) // 16]))
             return [got[:, c:c + NB] for c in range(0, count, NB)]
 
-        gw = {"c": gather("gw_c", U16, words, l_c, 0, E, "gw_c"),
-              "n": gather("gw_n0", U16, words, l_n, 0, NB, "gw_n0")}
-        gs = {"c": gather("gs_c", U8, scales, l_c, 0, E, "gs_c")}
-        quant((("c", 0), ("c", 1)))
-        gs["n"] = gather("gs_n0", U8, scales, l_n, 0, NB, "raw_c0")
-        quant((("n", 0), ("n", 1)))
-        gs["n"] = gs["n"] + gather("gs_n1", U8, scales, l_n, NB, NB, "raw_n0")
-        quant((("c", 2), ("n", 2)))
-        gw["n"] = gw["n"] + gather("gw_n1", U16, words, l_n, NB, NB, "raw_n2")
-        quant((("c", 3), ("n", 3)))
+        gs = {"c": gather("gs_c", U8, scales, l_c, 0, E, "gs_c"),
+              "n": gather("gs_n0", U8, scales, l_n, 0, NB, "gs_n0")}
+        gw = {"c": gather("gw_c", U16, words, l_c, 0, E, "gw_c")}
+        quant(0)
+        gw["n"] = gather("gw_n0", U16, words, l_n, 0, NB, "raw_n0")
+        quant(1)
+        gs["n"] = gs["n"] + gather("gs_n1", U8, scales, l_n, NB, NB, "raw_c1")
+        quant(2)
+        gw["n"] = gw["n"] + gather("gw_n1", U16, words, l_n, NB, NB, None)
+        quant(3)
 
         banks = {}
         reuse = {(1, 1): (2, 0)}
@@ -100,7 +106,7 @@ def tile_attend_edgeconv_kernel(tc, pts_words, pts_scales, wc, wn, bias, offs, o
                                 rhs_scale=gs[nm][e],
                                 start=(nm == "c"), stop=(nm == "n"))
 
-        for nm, m, e in (("c", 0, 0), ("c", 1, 0), ("c", 0, 1), ("n", 0, 0), ("n", 1, 0),
+        for nm, m, e in (("c", 0, 0), ("c", 0, 1), ("n", 0, 0), ("c", 1, 0), ("n", 1, 0),
                          ("c", 2, 0), ("n", 2, 0), ("c", 2, 1), ("n", 0, 1), ("n", 2, 1),
                          ("c", 3, 0), ("n", 3, 0), ("c", 3, 1), ("n", 3, 1)):
             mm(nm, m, e)
@@ -114,7 +120,7 @@ def tile_attend_edgeconv_kernel(tc, pts_words, pts_scales, wc, wn, bias, offs, o
 
         acts, steps, pairs = [], [], []
         for m in (0, 1):
-            act = sb.tile([P, 2, HALF], F32, name="act%d" % m)
+            act = late.tile([P, 2, HALF], F32, name="act%d" % m, align_bytes=64, offset=(4 * NB, 10 * NB)[m])
             nc.scalar.activation(act[:].rearrange("p h (g j) -> p h g j", j=DEG // 2),
                                  banks[m, 0][:].rearrange("p (g h j) -> p h g j", h=2, j=DEG // 2),
                                  relu, bias=bias_sb[:, m:m + 1])
@@ -130,7 +136,7 @@ def tile_attend_edgeconv_kernel(tc, pts_words, pts_scales, wc, wn, bias, offs, o
             nc.gpsimd.tensor_tensor(pair[:], acts[m][:, 0, :], steps[m][:], mybir.AluOpType.add)
             pairs.append(pair)
 
-        best = sb.tile([P, 4 * G], F32, name="best", tag="raw_n3", align_bytes=64)
+        best = late.tile([P, 4 * G], F32, name="best", align_bytes=64, offset=8 * NB)
         res = sb.tile([P, 4 * G], F32, name="res", tag="diff1", align_bytes=64)
         for m, e in ((2, 0), (0, 1), (2, 1), (3, 0), (3, 1), (1, 1)):
             if (m, e) in reuse:

@@ -16,6 +16,7 @@ K, T, E, F, G = 512, 2048, 1024, 512, 64
 DEG = E // G
 NB = 512
 GH = NB // DEG
+CH = 4 * P * 4
 FLOPS = 2 * 2 * K * F * E
 
 
@@ -30,68 +31,83 @@ def tile_attend_edgeconv_kernel(tc, pts_words, pts_scales, wc, wn, bias, offs, o
         l_n = sb.tile([P, E // 16], U16, name="l_n")
         words = sb.tile([P, 2 * T], U16, name="words", tag="words", align_bytes=64)
         scales = sb.tile([P, T], U8, name="scales", align_bytes=64)
-        bias_sb = sb.tile([P, F // P], F32, name="bias_sb")
+        plane_c = sb.tile([P, E], U8, name="plane_c", align_bytes=64)
+        at = {"c1": 0, "n2": 2 * CH, "bias": 4 * CH, "c3": 4 * CH + 64}
+        spread = late.tile([P, T], U8, name="spread", align_bytes=64, offset=2 * CH - T // 2)
+        got_c = late.tile([P, E], U8, name="got_c", align_bytes=64, offset=4 * CH)
 
         raw = {}
 
         def load(nm, m0, mt):
             w = wc if nm == "c" else wn
-            if m0 >= 2:
-                tile = late.tile([P, 4, mt * P], F32, name="raw_%s%d" % (nm, m0), align_bytes=64, offset=(m0 - 2) * 8 * NB)
+            name = "%s%d" % (nm, m0)
+            if name in at:
+                tile = late.tile([P, 4, mt * P], F32, name="raw_" + name, align_bytes=64, offset=at[name])
             else:
-                tile = sb.tile([P, 4, mt * P], F32, name="raw_%s%d" % (nm, m0), tag="raw_%s%d" % (nm, m0), align_bytes=64)
+                tile = sb.tile([P, 4, mt * P], F32, name="raw_" + name, tag="raw_" + name, align_bytes=64)
             nc.sync.dma_start(tile[:], w.rearrange("(p j) f -> p j f", j=4)[:, :, m0 * P:(m0 + mt) * P])
             for a in range(mt):
                 raw[nm, m0 + a] = tile[:, :, a * P:(a + 1) * P]
 
+        nc.vector.memset(spread[:].bitcast(I32), 0)
         nc.vector.memset(scales[:].bitcast(I32), 0)
         nc.vector.memset(words[:, T:].bitcast(I32), 0)
+        nc.vector.memset(plane_c[:].bitcast(I32), 0)
         load("c", 0, 1)
         nc.sync.dma_start(l_c[:], offs2)
+        nc.sync.dma_start(spread[0:P:8, :].bitcast(I32), pts_scales[0].bitcast(I32))
+        nc.sync.dma_start(l_n[:], offs)
+        nc.sync.dma_start(words[:, :T].bitcast(I32), pts_words[0].bitcast(I32))
         srows = pts_scales[0].bitcast(I32).rearrange("(q r) c -> r q c", r=4)
         for r in range(4):
             nc.sync.dma_start(scales[r:P:32, :].bitcast(I32), srows[r])
-        nc.sync.dma_start(l_n[:], offs)
-        nc.sync.dma_start(words[:, :T].bitcast(I32), pts_words[0].bitcast(I32))
-        for nm, m0, mt in (("n", 0, 2), ("c", 1, 2), ("n", 2, 2), ("c", 3, 1)):
+        load("n", 0, 2)
+
+        nc.vector.tensor_copy(got_c[:], spread[:].indirect(l_c[:]))
+        for r in range(4):
+            nc.sync.dma_start(plane_c[r:P:32, :].bitcast(I32), got_c[8 * r:P:32, :].bitcast(I32))
+        for nm, m0, mt in (("c", 1, 2), ("n", 2, 2), ("c", 3, 1)):
             load(nm, m0, mt)
+        bias_sb = late.tile([P, F // P], F32, name="bias_sb", align_bytes=64, offset=at["bias"])
         with nc.allow_non_contiguous_dma(reason="one bias value a partition"):
             nc.sync.dma_start(bias_sb[:], bias.rearrange("(m p) o -> p (m o)", p=P))
 
         codes = {}
         planes = {}
 
-        def quant(m):
-            grp = sb.tile([P, 2 * P, 4], BF16, name="grp%d" % m, align_bytes=64)
-            for a, nm in enumerate("cn"):
+        def quant(*parts):
+            name = "".join("%s%d" % part for part in parts)
+            n = len(parts) * P
+            grp = sb.tile([P, n, 4], BF16, name="grp" + name, align_bytes=64)
+            for a, part in enumerate(parts):
                 nc.scalar.copy(grp[:, a * P:(a + 1) * P, :].rearrange("p (c i) t -> p c t i", i=4),
-                               raw[nm, m].rearrange("p t (c i) -> p c t i", i=4))
-            cd = sb.tile([P, 2 * P], U32, name="codes%d" % m, align_bytes=64)
-            pl = sb.tile([P, 2 * P], U8, name="planes%d" % m, align_bytes=64)
+                               raw[part].rearrange("p t (c i) -> p c t i", i=4))
+            cd = sb.tile([P, n], U32, name="codes" + name, align_bytes=64)
+            pl = sb.tile([P, n], U8, name="planes" + name, align_bytes=64)
             nc.vector.quantize_mx(out=cd[:].bitcast(FP8X4), scales=pl[:],
                                   in_=grp[:].rearrange("p c t -> p (c t)"))
-            for a, nm in enumerate("cn"):
-                codes[nm, m] = cd[:, a * P:(a + 1) * P]
-                planes[nm, m] = pl[:, a * P:(a + 1) * P]
+            for a, part in enumerate(parts):
+                codes[part] = cd[:, a * P:(a + 1) * P]
+                planes[part] = pl[:, a * P:(a + 1) * P]
 
         def gather(name, dtype, window, lst, first, count, tag):
-            if tag is None:
-                got = late.tile([P, count], dtype, name=name, align_bytes=64, offset=0)
+            if tag in at:
+                got = late.tile([P, count], dtype, name=name, align_bytes=64, offset=at[tag] + (0 if tag == "c1" else CH // 2))
             else:
                 got = sb.tile([P, count], dtype, name=name, tag=tag, align_bytes=64)
             nc.vector.tensor_copy(got[:], window[:].indirect(lst[:, first // 16:(first + count) // 16]))
             return [got[:, c:c + NB] for c in range(0, count, NB)]
 
-        gs = {"c": gather("gs_c", U8, scales, l_c, 0, E, "gs_c"),
-              "n": gather("gs_n0", U8, scales, l_n, 0, NB, "gs_n0")}
+        gs = {"c": [plane_c[:, :NB], plane_c[:, NB:]]}
         gw = {"c": gather("gw_c", U16, words, l_c, 0, E, "gw_c")}
-        quant(0)
+        gs["n"] = gather("gs_n0", U8, scales, l_n, 0, NB, "gs_n0")
+        quant(("c", 0), ("n", 0))
         gw["n"] = gather("gw_n0", U16, words, l_n, 0, NB, "raw_n0")
-        quant(1)
-        gs["n"] = gs["n"] + gather("gs_n1", U8, scales, l_n, NB, NB, "raw_c1")
-        quant(2)
-        gw["n"] = gw["n"] + gather("gw_n1", U16, words, l_n, NB, NB, None)
-        quant(3)
+        quant(("c", 1), ("n", 1))
+        gs["n"] = gs["n"] + gather("gs_n1", U8, scales, l_n, NB, NB, "c1")
+        quant(("c", 2), ("n", 2))
+        gw["n"] = gw["n"] + gather("gw_n1", U16, words, l_n, NB, NB, "n2")
+        quant(("c", 3), ("n", 3))
 
         banks = {}
         reuse = {(1, 1): (2, 0)}
@@ -120,7 +136,7 @@ def tile_attend_edgeconv_kernel(tc, pts_words, pts_scales, wc, wn, bias, offs, o
 
         acts, steps, pairs = [], [], []
         for m in (0, 1):
-            act = late.tile([P, 2, HALF], F32, name="act%d" % m, align_bytes=64, offset=(4 * NB, 10 * NB)[m])
+            act = late.tile([P, 2, HALF], F32, name="act%d" % m, align_bytes=64, offset=(at["n2"] + CH, at["c3"] + CH // 2)[m])
             nc.scalar.activation(act[:].rearrange("p h (g j) -> p h g j", j=DEG // 2),
                                  banks[m, 0][:].rearrange("p (g h j) -> p h g j", h=2, j=DEG // 2),
                                  relu, bias=bias_sb[:, m:m + 1])
@@ -136,7 +152,7 @@ def tile_attend_edgeconv_kernel(tc, pts_words, pts_scales, wc, wn, bias, offs, o
             nc.gpsimd.tensor_tensor(pair[:], acts[m][:, 0, :], steps[m][:], mybir.AluOpType.add)
             pairs.append(pair)
 
-        best = late.tile([P, 4 * G], F32, name="best", align_bytes=64, offset=8 * NB)
+        best = late.tile([P, 4 * G], F32, name="best", align_bytes=64, offset=at["c3"])
         res = sb.tile([P, 4 * G], F32, name="res", tag="diff1", align_bytes=64)
         for m, e in ((2, 0), (0, 1), (2, 1), (3, 0), (3, 1), (1, 1)):
             if (m, e) in reuse:

@@ -27,14 +27,12 @@ def tile_attend_edgeconv_kernel(tc, pts_words, pts_scales, wc, wn, bias, offs, o
         late = ctx.enter_context(tc.tile_pool(name="late", bufs=1))
         ps = ctx.enter_context(tc.psum_pool(name="ps", bufs=1))
 
-        l_c = sb.tile([P, E // 16], U16, name="l_c")
-        l_n = sb.tile([P, E // 16], U16, name="l_n")
+        lists = {"c": sb.tile([P, E // 16], U16, name="l_c"), "n": sb.tile([P, E // 16], U16, name="l_n")}
         words = sb.tile([P, 2 * T], U16, name="words", tag="words", align_bytes=64)
-        scales = sb.tile([P, T], U8, name="scales", align_bytes=64)
-        plane_c = sb.tile([P, E], U8, name="plane_c", align_bytes=64)
-        at = {"c1": 0, "n2": 2 * CH, "bias": 4 * CH, "c3": 4 * CH + 64}
-        spread = late.tile([P, T], U8, name="spread", align_bytes=64, offset=2 * CH - T // 2)
-        got_c = late.tile([P, E], U8, name="got_c", align_bytes=64, offset=4 * CH)
+        at = {"n0": 0, "n2": 2 * CH, "c3": 5 * CH, "bias": 6 * CH}
+        spread = {"c": late.tile([P, T], U8, name="spread_c", align_bytes=64, offset=2 * CH - T // 2),
+                  "n": late.tile([P, T], U8, name="spread_n", align_bytes=64, offset=6 * CH - T // 2)}
+        plane = {nm: sb.tile([P, E], U8, name="plane_" + nm, align_bytes=64) for nm in "cn"}
 
         raw = {}
 
@@ -49,28 +47,21 @@ def tile_attend_edgeconv_kernel(tc, pts_words, pts_scales, wc, wn, bias, offs, o
             for a in range(mt):
                 raw[nm, m0 + a] = tile[:, :, a * P:(a + 1) * P]
 
-        nc.vector.memset(spread[:].bitcast(I32), 0)
-        nc.vector.memset(scales[:].bitcast(I32), 0)
-        nc.vector.memset(words[:, T:].bitcast(I32), 0)
-        nc.vector.memset(plane_c[:].bitcast(I32), 0)
-        load("c", 0, 1)
-        nc.sync.dma_start(l_c[:], offs2)
-        nc.sync.dma_start(spread[0:P:8, :].bitcast(I32), pts_scales[0].bitcast(I32))
-        nc.sync.dma_start(l_n[:], offs)
-        nc.sync.dma_start(words[:, :T].bitcast(I32), pts_words[0].bitcast(I32))
-        srows = pts_scales[0].bitcast(I32).rearrange("(q r) c -> r q c", r=4)
-        for r in range(4):
-            nc.sync.dma_start(scales[r:P:32, :].bitcast(I32), srows[r])
-        load("n", 0, 2)
+        def gather_scales(nm):
+            got = sb.tile([P, E], U8, name="got_" + nm, align_bytes=64)
+            nc.vector.tensor_copy(got[:], spread[nm][:].indirect(lists[nm][:]))
+            for r in range(4):
+                nc.sync.dma_start(plane[nm][r:P:32, :].bitcast(I32), got[8 * r:P:32, :].bitcast(I32))
 
-        nc.vector.tensor_copy(got_c[:], spread[:].indirect(l_c[:]))
-        for r in range(4):
-            nc.sync.dma_start(plane_c[r:P:32, :].bitcast(I32), got_c[8 * r:P:32, :].bitcast(I32))
-        for nm, m0, mt in (("c", 1, 2), ("n", 2, 2), ("c", 3, 1)):
-            load(nm, m0, mt)
-        bias_sb = late.tile([P, F // P], F32, name="bias_sb", align_bytes=64, offset=at["bias"])
-        with nc.allow_non_contiguous_dma(reason="one bias value a partition"):
-            nc.sync.dma_start(bias_sb[:], bias.rearrange("(m p) o -> p (m o)", p=P))
+        for tile in (spread["c"][:], spread["n"][:], words[:, T:], plane["c"][:], plane["n"][:]):
+            nc.vector.memset(tile.bitcast(I32), 0)
+        load("c", 0, 1)
+        nc.sync.dma_start(lists["c"][:], offs2)
+        nc.sync.dma_start(spread["c"][0:P:8, :].bitcast(I32), pts_scales[0].bitcast(I32))
+        nc.sync.dma_start(words[:, :T].bitcast(I32), pts_words[0].bitcast(I32))
+        nc.sync.dma_start(lists["n"][:], offs)
+        nc.sync.dma_start(spread["n"][0:P:8, :].bitcast(I32), pts_scales[0].bitcast(I32))
+        load("c", 1, 2)
 
         codes = {}
         planes = {}
@@ -78,7 +69,7 @@ def tile_attend_edgeconv_kernel(tc, pts_words, pts_scales, wc, wn, bias, offs, o
         def quant(*parts):
             name = "".join("%s%d" % part for part in parts)
             n = len(parts) * P
-            grp = sb.tile([P, n, 4], BF16, name="grp" + name, align_bytes=64)
+            grp = sb.tile([P, n, 4], BF16, name="grp" + name, tag="grp" + name, align_bytes=64)
             for a, part in enumerate(parts):
                 nc.scalar.copy(grp[:, a * P:(a + 1) * P, :].rearrange("p (c i) t -> p c t i", i=4),
                                raw[part].rearrange("p t (c i) -> p c t i", i=4))
@@ -90,81 +81,103 @@ def tile_attend_edgeconv_kernel(tc, pts_words, pts_scales, wc, wn, bias, offs, o
                 codes[part] = cd[:, a * P:(a + 1) * P]
                 planes[part] = pl[:, a * P:(a + 1) * P]
 
-        def gather(name, dtype, window, lst, first, count, tag):
+        def gather_words(name, nm, first, count, tag):
             if tag in at:
-                got = late.tile([P, count], dtype, name=name, align_bytes=64, offset=at[tag] + (0 if tag == "c1" else CH // 2))
+                got = late.tile([P, count], U16, name=name, align_bytes=64, offset=at[tag])
             else:
-                got = sb.tile([P, count], dtype, name=name, tag=tag, align_bytes=64)
-            nc.vector.tensor_copy(got[:], window[:].indirect(lst[:, first // 16:(first + count) // 16]))
+                got = sb.tile([P, count], U16, name=name, tag=tag, align_bytes=64)
+            nc.vector.tensor_copy(got[:], words[:].indirect(lists[nm][:, first // 16:(first + count) // 16]))
             return [got[:, c:c + NB] for c in range(0, count, NB)]
 
-        gs = {"c": [plane_c[:, :NB], plane_c[:, NB:]]}
-        gw = {"c": gather("gw_c", U16, words, l_c, 0, E, "gw_c")}
-        gs["n"] = gather("gs_n0", U8, scales, l_n, 0, NB, "gs_n0")
-        quant(("c", 0), ("n", 0))
-        gw["n"] = gather("gw_n0", U16, words, l_n, 0, NB, "raw_n0")
-        quant(("c", 1), ("n", 1))
-        gs["n"] = gs["n"] + gather("gs_n1", U8, scales, l_n, NB, NB, "c1")
-        quant(("c", 2), ("n", 2))
-        gw["n"] = gw["n"] + gather("gw_n1", U16, words, l_n, NB, NB, "n2")
-        quant(("c", 3), ("n", 3))
+        gather_scales("c")
+        load("n", 0, 2)
+        load("n", 2, 2)
+        gw = {"c": gather_words("gw_c", "c", 0, E, "gw_c")}
+        quant(("c", 0))
+        gather_scales("n")
+        bias_sb = late.tile([P, F // P], F32, name="bias_sb", align_bytes=64, offset=at["bias"])
+        with nc.allow_non_contiguous_dma(reason="one bias value a partition"):
+            nc.sync.dma_start(bias_sb[:], bias.rearrange("(m p) o -> p (m o)", p=P))
+        load("c", 3, 1)
+        quant(("c", 1), ("c", 2))
+        gw["n"] = gather_words("gw_n0", "n", 0, NB, "raw_c1")
+        quant(("n", 0), ("n", 1))
+        gw["n"] = gw["n"] + gather_words("gw_n1", "n", NB, NB, "n0")
+        quant(("n", 2), ("n", 3))
 
         banks = {}
-        reuse = {(1, 1): (2, 0)}
 
         def mm(nm, m, e):
             if nm == "c":
-                banks[m, e] = ps.tile([P, NB], F32, name="bank_%d%d" % (m, e), tag="bank_%d%d" % reuse.get((m, e), (m, e)))
+                banks[m, e] = ps.tile([P, NB], F32, name="bank_%d%d" % (m, e))
             nc.tensor.matmul_mx(out=banks[m, e][:],
                                 lhsT=codes[nm, m].bitcast(FP8X4),
                                 lhsT_scale=planes[nm, m],
                                 rhs=gw[nm][e].bitcast(FP4X4),
-                                rhs_scale=gs[nm][e],
+                                rhs_scale=plane[nm][:, e * NB:(e + 1) * NB],
                                 start=(nm == "c"), stop=(nm == "n"))
 
-        for nm, m, e in (("c", 0, 0), ("c", 0, 1), ("n", 0, 0), ("c", 1, 0), ("n", 1, 0),
-                         ("c", 2, 0), ("n", 2, 0), ("c", 2, 1), ("n", 0, 1), ("n", 2, 1),
-                         ("c", 3, 0), ("n", 3, 0), ("c", 3, 1), ("n", 3, 1)):
-            mm(nm, m, e)
+        for m in range(3):
+            for e in (0, 1):
+                mm("c", m, e)
+        for m, e in ((0, 0), (1, 0), (1, 1), (0, 1), (2, 0), (2, 1)):
+            mm("n", m, e)
 
         relu = mybir.ActivationFunctionType.Relu
-        HALF = NB // 2
+        share = (GH, 24)
 
         def group_max(dst, src, width):
             nc.vector.tensor_reduce(out=dst, in_=src.rearrange("p (g j) -> p g j", j=width),
                                     axis=mybir.AxisListType.X, op=mybir.AluOpType.max)
 
-        acts, steps, pairs = [], [], []
-        for m in (0, 1):
-            act = late.tile([P, 2, HALF], F32, name="act%d" % m, align_bytes=64, offset=(at["n2"] + CH, at["c3"] + CH // 2)[m])
+        def empty(e, offset):
+            act = late.tile([P, 2, share[e] * DEG // 2], F32, name="act%d" % e, align_bytes=64, offset=offset)
             nc.scalar.activation(act[:].rearrange("p h (g j) -> p h g j", j=DEG // 2),
-                                 banks[m, 0][:].rearrange("p (g h j) -> p h g j", h=2, j=DEG // 2),
-                                 relu, bias=bias_sb[:, m:m + 1])
-            acts.append(act)
-        for m, act in enumerate(acts):
-            diff = sb.tile([P, HALF], F32, name="diff%d" % m, tag=("words", "diff1")[m], align_bytes=64)
+                                 banks[0, e][:, :share[e] * DEG].rearrange("p (g h j) -> p h g j", h=2, j=DEG // 2),
+                                 relu, bias=bias_sb[:, 0:1])
+            return act
+
+        best = {}
+
+        def direct(m, offset):
+            best[m] = late.tile([P, G], F32, name="best%d" % m, align_bytes=64, offset=offset)
+            for e in (0, 1):
+                group_max(best[m][:, e * GH:(e + 1) * GH], banks[m, e][:], DEG)
+
+        def finish(m):
+            nc.scalar.activation(res[:, m * G:(m + 1) * G], best[m][:], relu, bias=bias_sb[:, m:m + 1])
+
+        acts = [empty(0, at["n2"] + CH)]
+        direct(1, at["n2"] + CH // 2)
+        quant(("c", 3))
+        for e in (0, 1):
+            mm("c", 3, e)
+            mm("n", 3, e)
+        acts.append(empty(1, at["c3"] + 64 - 1536))
+        steps, pairs = [], []
+        for e, act in enumerate(acts):
+            diff = sb.tile([P, share[e] * DEG // 2], F32, name="diff%d" % e, tag=("grpn2n3", "grpc3")[e], align_bytes=64)
             nc.gpsimd.tensor_tensor(diff[:], act[:, 1, :], act[:, 0, :], mybir.AluOpType.subtract)
-            step = sb.tile([P, HALF], F32, name="step%d" % m)
+            step = late.tile([P, share[e] * DEG // 2], F32, name="step%d" % e, align_bytes=64, offset=(at["c3"] + 64, 7 * CH)[e])
             nc.scalar.activation(step[:], diff[:], relu)
             steps.append(step)
-        for m in (0, 1):
-            pair = sb.tile([P, HALF], F32, name="pair%d" % m)
-            nc.gpsimd.tensor_tensor(pair[:], acts[m][:, 0, :], steps[m][:], mybir.AluOpType.add)
+        for e in (0, 1):
+            pair = sb.tile([P, share[e] * DEG // 2], F32, name="pair%d" % e)
+            nc.gpsimd.tensor_tensor(pair[:], acts[e][:, 0, :], steps[e][:], mybir.AluOpType.add)
             pairs.append(pair)
 
-        best = late.tile([P, 4 * G], F32, name="best", align_bytes=64, offset=at["c3"])
-        res = sb.tile([P, 4 * G], F32, name="res", tag="diff1", align_bytes=64)
-        for m, e in ((2, 0), (0, 1), (2, 1), (3, 0), (3, 1), (1, 1)):
-            if (m, e) in reuse:
-                mm("c", m, e)
-                mm("n", m, e)
-            group_max(best[:, m * G + e * GH:m * G + (e + 1) * GH], banks[m, e][:], DEG)
-            if e == 1:
-                first = m * G + (GH if m < 2 else 0)
-                nc.scalar.activation(res[:, first:(m + 1) * G], best[:, first:(m + 1) * G], relu, bias=bias_sb[:, m:m + 1])
-            if (m, e) == (3, 1):
-                nc.sync.dma_start(out[2 * P:, :].rearrange("(m p) g -> p m g", p=P),
-                                  res[:, 2 * G:].rearrange("p (m g) -> p m g", g=G))
-        for m in (0, 1):
-            group_max(res[:, m * G:m * G + GH], pairs[m][:], DEG // 2)
-            nc.sync.dma_start(out[m * P:(m + 1) * P, :], res[:, m * G:(m + 1) * G])
+        res = sb.tile([P, 4 * G], F32, name="res", tag="grpn2n3", align_bytes=64)
+        finish(1)
+        direct(2, at["c3"] + 64 + CH // 2)
+        finish(2)
+        nc.sync.dma_start(out[P:3 * P, :].rearrange("(m p) g -> p m g", p=P),
+                          res[:, G:3 * G].rearrange("p (m g) -> p m g", g=G))
+        rest = late.tile([P, GH - share[1]], F32, name="rest", align_bytes=64, offset=at["c3"] + 64 + CH // 2 + 8 * G)
+        group_max(rest[:], banks[0, 1][:, share[1] * DEG:], DEG)
+        nc.scalar.activation(res[:, GH + share[1]:G], rest[:], relu, bias=bias_sb[:, 0:1])
+        direct(3, at["c3"] + 64 + CH // 2 + 4 * G)
+        finish(3)
+        nc.sync.dma_start(out[3 * P:, :], res[:, 3 * G:])
+        for e in (0, 1):
+            group_max(res[:, e * GH:e * GH + share[e]], pairs[e][:], DEG // 2)
+        nc.sync.dma_start(out[:P, :], res[:, :G])

@@ -30,7 +30,7 @@ def tile_attend_edgeconv_kernel(tc, pts_words, pts_scales, wc, wn, bias, offs, o
         lists = {"c": sb.tile([P, E // 16], U16, name="l_c"), "n": sb.tile([P, E // 16], U16, name="l_n")}
         words = sb.tile([P, 2 * T], U16, name="words", tag="words", align_bytes=64)
         at = {"n0": 0, "n2": 2 * CH, "c3": 5 * CH, "bias": 6 * CH}
-        spread = {"c": late.tile([P, T], U8, name="spread_c", align_bytes=64, offset=2 * CH - T // 2),
+        spread = {"c": late.tile([P, T], U8, name="spread_c", align_bytes=64, offset=2 * CH),
                   "n": late.tile([P, T], U8, name="spread_n", align_bytes=64, offset=6 * CH - T // 2)}
         plane = {nm: sb.tile([P, E], U8, name="plane_" + nm, align_bytes=64) for nm in "cn"}
 
@@ -62,6 +62,7 @@ def tile_attend_edgeconv_kernel(tc, pts_words, pts_scales, wc, wn, bias, offs, o
         nc.sync.dma_start(lists["n"][:], offs)
         nc.sync.dma_start(spread["n"][0:P:8, :].bitcast(I32), pts_scales[0].bitcast(I32))
         load("c", 1, 2)
+        load("n", 0, 2)
 
         codes = {}
         planes = {}
@@ -90,15 +91,16 @@ def tile_attend_edgeconv_kernel(tc, pts_words, pts_scales, wc, wn, bias, offs, o
             return [got[:, c:c + NB] for c in range(0, count, NB)]
 
         gather_scales("c")
-        load("n", 0, 2)
         load("n", 2, 2)
         gw = {"c": gather_words("gw_c", "c", 0, E, "gw_c")}
         quant(("c", 0))
         gather_scales("n")
-        bias_sb = late.tile([P, F // P], F32, name="bias_sb", align_bytes=64, offset=at["bias"])
+        bias_0 = late.tile([P, 1], F32, name="bias_0", align_bytes=64, offset=at["bias"])
+        bias_r = late.tile([P, F // P - 1], F32, name="bias_r", align_bytes=64, offset=at["bias"] + 64)
         with nc.allow_non_contiguous_dma(reason="one bias value a partition"):
-            nc.sync.dma_start(bias_sb[:], bias.rearrange("(m p) o -> p (m o)", p=P))
-        load("c", 3, 1)
+            nc.sync.dma_start(bias_0[:], bias[:P, :])
+            load("c", 3, 1)
+            nc.sync.dma_start(bias_r[:], bias[P:, :].rearrange("(m p) o -> p (m o)", p=P))
         quant(("c", 1), ("c", 2))
         gw["n"] = gather_words("gw_n0", "n", 0, NB, "raw_c1")
         quant(("n", 0), ("n", 1))
@@ -134,7 +136,7 @@ def tile_attend_edgeconv_kernel(tc, pts_words, pts_scales, wc, wn, bias, offs, o
             act = late.tile([P, 2, share[e] * DEG // 2], F32, name="act%d" % e, align_bytes=64, offset=offset)
             nc.scalar.activation(act[:].rearrange("p h (g j) -> p h g j", j=DEG // 2),
                                  banks[0, e][:, :share[e] * DEG].rearrange("p (g h j) -> p h g j", h=2, j=DEG // 2),
-                                 relu, bias=bias_sb[:, 0:1])
+                                 relu, bias=bias_0[:])
             return act
 
         best = {}
@@ -145,7 +147,7 @@ def tile_attend_edgeconv_kernel(tc, pts_words, pts_scales, wc, wn, bias, offs, o
                 group_max(best[m][:, e * GH:(e + 1) * GH], banks[m, e][:], DEG)
 
         def finish(m):
-            nc.scalar.activation(res[:, m * G:(m + 1) * G], best[m][:], relu, bias=bias_sb[:, m:m + 1])
+            nc.scalar.activation(res[:, m * G:(m + 1) * G], best[m][:], relu, bias=bias_r[:, m - 1:m])
 
         acts = [empty(0, at["n2"] + CH)]
         direct(1, at["n2"] + CH // 2)
@@ -174,7 +176,7 @@ def tile_attend_edgeconv_kernel(tc, pts_words, pts_scales, wc, wn, bias, offs, o
                           res[:, G:3 * G].rearrange("p (m g) -> p m g", g=G))
         rest = late.tile([P, GH - share[1]], F32, name="rest", align_bytes=64, offset=at["c3"] + 64 + CH // 2 + 8 * G)
         group_max(rest[:], banks[0, 1][:, share[1] * DEG:], DEG)
-        nc.scalar.activation(res[:, GH + share[1]:G], rest[:], relu, bias=bias_sb[:, 0:1])
+        nc.scalar.activation(res[:, GH + share[1]:G], rest[:], relu, bias=bias_0[:])
         direct(3, at["c3"] + 64 + CH // 2 + 4 * G)
         finish(3)
         nc.sync.dma_start(out[3 * P:, :], res[:, 3 * G:])

@@ -29,9 +29,9 @@ def tile_attend_edgeconv_kernel(tc, pts_words, pts_scales, wc, wn, bias, offs, o
 
         lists = {"c": sb.tile([P, E // 16], U16, name="l_c"), "n": sb.tile([P, E // 16], U16, name="l_n")}
         words = sb.tile([P, 2 * T], U16, name="words", tag="words", align_bytes=64)
-        at = {"n0": 0, "n2": 2 * CH, "c3": 5 * CH, "bias": 6 * CH}
-        spread = {"c": late.tile([P, T], U8, name="spread_c", align_bytes=64, offset=2 * CH),
-                  "n": late.tile([P, T], U8, name="spread_n", align_bytes=64, offset=6 * CH - T // 2)}
+        at = {"n0": 0, "n2": 2 * CH, "c3": 4 * CH, "bias": 6 * CH}
+        spread = {"c": late.tile([P, T], U8, name="spread_c", align_bytes=64, offset=4 * CH - T // 2),
+                  "n": late.tile([P, T], U8, name="spread_n", align_bytes=64, offset=6 * CH)}
         plane = {nm: sb.tile([P, E], U8, name="plane_" + nm, align_bytes=64) for nm in "cn"}
 
         raw = {}
@@ -92,26 +92,26 @@ def tile_attend_edgeconv_kernel(tc, pts_words, pts_scales, wc, wn, bias, offs, o
 
         gather_scales("c")
         load("n", 2, 2)
+        load("c", 3, 1)
         gw = {"c": gather_words("gw_c", "c", 0, E, "gw_c")}
         quant(("c", 0))
         gather_scales("n")
-        bias_0 = late.tile([P, 1], F32, name="bias_0", align_bytes=64, offset=at["bias"])
-        bias_r = late.tile([P, F // P - 1], F32, name="bias_r", align_bytes=64, offset=at["bias"] + 64)
+        bias_sb = late.tile([P, F // P], F32, name="bias_sb", align_bytes=64, offset=at["bias"])
         with nc.allow_non_contiguous_dma(reason="one bias value a partition"):
-            nc.sync.dma_start(bias_0[:], bias[:P, :])
-            load("c", 3, 1)
-            nc.sync.dma_start(bias_r[:], bias[P:, :].rearrange("(m p) o -> p (m o)", p=P))
+            nc.sync.dma_start(bias_sb[:], bias.rearrange("(m p) o -> p (m o)", p=P))
         quant(("c", 1), ("c", 2))
         gw["n"] = gather_words("gw_n0", "n", 0, NB, "raw_c1")
         quant(("n", 0), ("n", 1))
         gw["n"] = gw["n"] + gather_words("gw_n1", "n", NB, NB, "n0")
         quant(("n", 2), ("n", 3))
+        quant(("c", 3))
 
         banks = {}
+        reuse = {(3, 0): (1, 0), (3, 1): (0, 0)}
 
         def mm(nm, m, e):
             if nm == "c":
-                banks[m, e] = ps.tile([P, NB], F32, name="bank_%d%d" % (m, e))
+                banks[m, e] = ps.tile([P, NB], F32, name="bank_%d%d" % (m, e), tag="bank_%d%d" % reuse.get((m, e), (m, e)))
             nc.tensor.matmul_mx(out=banks[m, e][:],
                                 lhsT=codes[nm, m].bitcast(FP8X4),
                                 lhsT_scale=planes[nm, m],
@@ -122,64 +122,44 @@ def tile_attend_edgeconv_kernel(tc, pts_words, pts_scales, wc, wn, bias, offs, o
         for m in range(3):
             for e in (0, 1):
                 mm("c", m, e)
-        for m, e in ((0, 0), (1, 0), (1, 1), (0, 1), (2, 0), (2, 1)):
+        for m, e in ((1, 0), (0, 0), (1, 1), (0, 1), (2, 0), (2, 1)):
             mm("n", m, e)
 
         relu = mybir.ActivationFunctionType.Relu
-        share = (GH, 24)
+        HALF = NB // 2
 
         def group_max(dst, src, width):
             nc.vector.tensor_reduce(out=dst, in_=src.rearrange("p (g j) -> p g j", j=width),
                                     axis=mybir.AxisListType.X, op=mybir.AluOpType.max)
 
-        def empty(e, offset):
-            act = late.tile([P, 2, share[e] * DEG // 2], F32, name="act%d" % e, align_bytes=64, offset=offset)
-            nc.scalar.activation(act[:].rearrange("p h (g j) -> p h g j", j=DEG // 2),
-                                 banks[0, e][:, :share[e] * DEG].rearrange("p (g h j) -> p h g j", h=2, j=DEG // 2),
-                                 relu, bias=bias_0[:])
-            return act
+        act = late.tile([P, 2, HALF], F32, name="act", align_bytes=64, offset=at["c3"] + CH // 2)
+        nc.scalar.activation(act[:].rearrange("p h (g j) -> p h g j", j=DEG // 2),
+                             banks[0, 0][:].rearrange("p (g h j) -> p h g j", h=2, j=DEG // 2),
+                             relu, bias=bias_sb[:, 0:1])
+        diff = sb.tile([P, HALF], F32, name="diff", tag="grpc3", align_bytes=64)
+        nc.gpsimd.tensor_tensor(diff[:], act[:, 1, :], act[:, 0, :], mybir.AluOpType.subtract)
+        step = sb.tile([P, HALF], F32, name="step", tag="step")
+        nc.scalar.activation(step[:], diff[:], relu)
+        act1 = sb.tile([P, NB], F32, name="act1", tag="grpc3", align_bytes=64)
+        nc.scalar.activation(act1[:], banks[0, 1][:], relu, bias=bias_sb[:, 0:1])
+        pair = sb.tile([P, HALF], F32, name="pair")
+        nc.gpsimd.tensor_tensor(pair[:], act[:, 0, :], step[:], mybir.AluOpType.add)
 
-        best = {}
-
-        def direct(m, offset):
-            best[m] = late.tile([P, G], F32, name="best%d" % m, align_bytes=64, offset=offset)
-            for e in (0, 1):
-                group_max(best[m][:, e * GH:(e + 1) * GH], banks[m, e][:], DEG)
-
-        def finish(m):
-            nc.scalar.activation(res[:, m * G:(m + 1) * G], best[m][:], relu, bias=bias_r[:, m - 1:m])
-
-        acts = [empty(0, at["n2"] + CH)]
-        direct(1, at["n2"] + CH // 2)
-        quant(("c", 3))
-        for e in (0, 1):
-            mm("c", 3, e)
-            mm("n", 3, e)
-        acts.append(empty(1, at["c3"] + 64 - 1536))
-        steps, pairs = [], []
-        for e, act in enumerate(acts):
-            diff = sb.tile([P, share[e] * DEG // 2], F32, name="diff%d" % e, tag=("grpn2n3", "grpc3")[e], align_bytes=64)
-            nc.gpsimd.tensor_tensor(diff[:], act[:, 1, :], act[:, 0, :], mybir.AluOpType.subtract)
-            step = late.tile([P, share[e] * DEG // 2], F32, name="step%d" % e, align_bytes=64, offset=(at["c3"] + 64, 7 * CH)[e])
-            nc.scalar.activation(step[:], diff[:], relu)
-            steps.append(step)
-        for e in (0, 1):
-            pair = sb.tile([P, share[e] * DEG // 2], F32, name="pair%d" % e)
-            nc.gpsimd.tensor_tensor(pair[:], acts[e][:, 0, :], steps[e][:], mybir.AluOpType.add)
-            pairs.append(pair)
-
-        res = sb.tile([P, 4 * G], F32, name="res", tag="grpn2n3", align_bytes=64)
-        finish(1)
-        direct(2, at["c3"] + 64 + CH // 2)
-        finish(2)
-        nc.sync.dma_start(out[P:3 * P, :].rearrange("(m p) g -> p m g", p=P),
-                          res[:, G:3 * G].rearrange("p (m g) -> p m g", g=G))
-        rest = late.tile([P, GH - share[1]], F32, name="rest", align_bytes=64, offset=at["c3"] + 64 + CH // 2 + 8 * G)
-        group_max(rest[:], banks[0, 1][:, share[1] * DEG:], DEG)
-        nc.scalar.activation(res[:, GH + share[1]:G], rest[:], relu, bias=bias_0[:])
-        direct(3, at["c3"] + 64 + CH // 2 + 4 * G)
-        finish(3)
-        nc.sync.dma_start(out[3 * P:, :], res[:, 3 * G:])
-        for e in (0, 1):
-            group_max(res[:, e * GH:e * GH + share[e]], pairs[e][:], DEG // 2)
-        nc.sync.dma_start(out[:P, :], res[:, :G])
+        best = late.tile([P, 4 * G], F32, name="best", align_bytes=64, offset=at["c3"])
+        res = sb.tile([P, 4 * G], F32, name="res", align_bytes=64)
+        res0 = late.tile([P, G], F32, name="res0", align_bytes=64, offset=at["n0"])
+        for m, e in ((1, 0), (1, 1), (2, 0), (2, 1), (3, 0), (3, 1)):
+            if (m, e) in reuse:
+                mm("c", m, e)
+                mm("n", m, e)
+            group_max(best[:, m * G + e * GH:m * G + (e + 1) * GH], banks[m, e][:], DEG)
+            if e == 1:
+                nc.scalar.activation(res[:, m * G:(m + 1) * G], best[:, m * G:(m + 1) * G], relu, bias=bias_sb[:, m:m + 1])
+            if (m, e) == (2, 1):
+                nc.sync.dma_start(out[P:3 * P, :].rearrange("(m p) g -> p m g", p=P),
+                                  res[:, G:3 * G].rearrange("p (m g) -> p m g", g=G))
+            if (m, e) == (3, 1):
+                nc.sync.dma_start(out[3 * P:, :], res[:, 3 * G:])
+        group_max(res0[:, GH:], act1[:], DEG)
+        group_max(res0[:, :GH], pair[:], DEG // 2)
+        nc.sync.dma_start(out[:P, :], res0[:])

@@ -132,34 +132,42 @@ def tile_attend_edgeconv_kernel(tc, pts_words, pts_scales, wc, wn, bias, offs, o
             nc.vector.tensor_reduce(out=dst, in_=src.rearrange("p (g j) -> p g j", j=width),
                                     axis=mybir.AxisListType.X, op=mybir.AluOpType.max)
 
-        act = late.tile([P, 2, HALF], F32, name="act", align_bytes=64, offset=at["c3"] + CH // 2)
-        nc.scalar.activation(act[:].rearrange("p h (g j) -> p h g j", j=DEG // 2),
-                             banks[0, 0][:].rearrange("p (g h j) -> p h g j", h=2, j=DEG // 2),
-                             relu, bias=bias_sb[:, 0:1])
-        diff = sb.tile([P, HALF], F32, name="diff", tag="grpc3", align_bytes=64)
-        nc.gpsimd.tensor_tensor(diff[:], act[:, 1, :], act[:, 0, :], mybir.AluOpType.subtract)
-        step = sb.tile([P, HALF], F32, name="step", tag="step")
-        nc.scalar.activation(step[:], diff[:], relu)
-        act1 = sb.tile([P, NB], F32, name="act1", tag="grpc3", align_bytes=64)
-        nc.scalar.activation(act1[:], banks[0, 1][:], relu, bias=bias_sb[:, 0:1])
-        pair = sb.tile([P, HALF], F32, name="pair")
-        nc.gpsimd.tensor_tensor(pair[:], act[:, 0, :], step[:], mybir.AluOpType.add)
+        share = (GH, 16)
+        acts, steps, pairs = [], [], []
+        for e in (0, 1):
+            act = late.tile([P, 2, HALF], F32, name="act%d" % e, align_bytes=64, offset=at["c3"] + (CH // 2, 64 - CH)[e])
+            nc.scalar.activation(act[:].rearrange("p h (g j) -> p h g j", j=DEG // 2),
+                                 banks[0, e][:].rearrange("p (g h j) -> p h g j", h=2, j=DEG // 2),
+                                 relu, bias=bias_sb[:, 0:1])
+            acts.append(act)
+        for e, act in enumerate(acts):
+            n = share[e] * DEG // 2
+            diff = sb.tile([P, n], F32, name="diff%d" % e, tag=("grpc3", "diff1")[e], align_bytes=64)
+            nc.gpsimd.tensor_tensor(diff[:], act[:, 1, :n], act[:, 0, :n], mybir.AluOpType.subtract)
+            step = sb.tile([P, n], F32, name="step%d" % e)
+            nc.scalar.activation(step[:], diff[:], relu)
+            steps.append(step)
+        for e, act in enumerate(acts):
+            n = share[e] * DEG // 2
+            pair = sb.tile([P, n], F32, name="pair%d" % e)
+            nc.gpsimd.tensor_tensor(pair[:], act[:, 0, :n], steps[e][:], mybir.AluOpType.add)
+            pairs.append(pair)
 
-        best = late.tile([P, 4 * G], F32, name="best", align_bytes=64, offset=at["c3"])
-        res = sb.tile([P, 4 * G], F32, name="res", align_bytes=64)
+        best = late.tile([P, 3 * G], F32, name="best", align_bytes=64, offset=at["c3"] + 64)
+        res = sb.tile([P, 3 * G], F32, name="res", tag="grpc3", align_bytes=64)
         res0 = late.tile([P, G], F32, name="res0", align_bytes=64, offset=at["n0"])
-        for m, e in ((1, 0), (1, 1), (2, 0), (2, 1), (3, 0), (3, 1)):
-            if (m, e) in reuse:
-                mm("c", m, e)
-                mm("n", m, e)
-            group_max(best[:, m * G + e * GH:m * G + (e + 1) * GH], banks[m, e][:], DEG)
-            if e == 1:
-                nc.scalar.activation(res[:, m * G:(m + 1) * G], best[:, m * G:(m + 1) * G], relu, bias=bias_sb[:, m:m + 1])
-            if (m, e) == (2, 1):
-                nc.sync.dma_start(out[P:3 * P, :].rearrange("(m p) g -> p m g", p=P),
-                                  res[:, G:3 * G].rearrange("p (m g) -> p m g", g=G))
-            if (m, e) == (3, 1):
-                nc.sync.dma_start(out[3 * P:, :], res[:, 3 * G:])
-        group_max(res0[:, GH:], act1[:], DEG)
-        group_max(res0[:, :GH], pair[:], DEG // 2)
-        nc.sync.dma_start(out[:P, :], res0[:])
+        for m in (1, 2, 3):
+            cols = slice((m - 1) * G, m * G)
+            for e in (0, 1):
+                if (m, e) in reuse:
+                    mm("c", m, e)
+                    mm("n", m, e)
+                group_max(best[:, cols][:, e * GH:(e + 1) * GH], banks[m, e][:], DEG)
+            nc.scalar.activation(res[:, cols], best[:, cols], relu, bias=bias_sb[:, m:m + 1])
+            nc.sync.dma_start(out[m * P:(m + 1) * P, :], res[:, cols])
+        nc.vector.tensor_reduce(out=res0[:, GH + share[1]:],
+                                in_=acts[1][:, :, share[1] * DEG // 2:].rearrange("p h (g j) -> p g h j", j=DEG // 2),
+                                axis=mybir.AxisListType.XY, op=mybir.AluOpType.max)
+        for e in (0, 1):
+            group_max(res0[:, e * GH:e * GH + share[e]], pairs[e][:], DEG // 2)
+            nc.sync.dma_start(out[:P, e * GH:(e + 1) * GH], res0[:, e * GH:(e + 1) * GH])

@@ -28,11 +28,10 @@ def tile_attend_edgeconv_kernel(tc, pts_words, pts_scales, wc, wn, bias, offs, o
         ps = ctx.enter_context(tc.psum_pool(name="ps", bufs=1))
 
         lists = {"c": sb.tile([P, E // 16], U16, name="l_c"), "n": sb.tile([P, E // 16], U16, name="l_n")}
-        words = sb.tile([P, 2 * T], U16, name="words", tag="words", align_bytes=64)
-        at = {"n0": 0, "n2": 2 * CH, "c3": 4 * CH, "bias": 6 * CH}
-        spread = {"c": late.tile([P, T], U8, name="spread_c", align_bytes=64, offset=4 * CH - T // 2),
-                  "n": late.tile([P, T], U8, name="spread_n", align_bytes=64, offset=6 * CH)}
+        words = sb.tile([P, 2 * T], U16, name="words", align_bytes=64)
+        table = sb.tile([P, T], U8, name="table", align_bytes=64)
         plane = {nm: sb.tile([P, E], U8, name="plane_" + nm, align_bytes=64) for nm in "cn"}
+        at = {"c0": 0, "n0": 4 * CH, "n3": 6 * CH}
 
         raw = {}
 
@@ -42,88 +41,96 @@ def tile_attend_edgeconv_kernel(tc, pts_words, pts_scales, wc, wn, bias, offs, o
             if name in at:
                 tile = late.tile([P, 4, mt * P], F32, name="raw_" + name, align_bytes=64, offset=at[name])
             else:
-                tile = sb.tile([P, 4, mt * P], F32, name="raw_" + name, tag="raw_" + name, align_bytes=64)
+                tile = sb.tile([P, 4, mt * P], F32, name="raw_" + name, align_bytes=64)
             nc.sync.dma_start(tile[:], w.rearrange("(p j) f -> p j f", j=4)[:, :, m0 * P:(m0 + mt) * P])
-            for a in range(mt):
-                raw[nm, m0 + a] = tile[:, :, a * P:(a + 1) * P]
+            raw[name] = tile
 
         def gather_scales(nm):
             got = sb.tile([P, E], U8, name="got_" + nm, align_bytes=64)
-            nc.vector.tensor_copy(got[:], spread[nm][:].indirect(lists[nm][:]))
-            for r in range(4):
-                nc.sync.dma_start(plane[nm][r:P:32, :].bitcast(I32), got[8 * r:P:32, :].bitcast(I32))
+            nc.vector.tensor_copy(got[:], table[:].indirect(lists[nm][:]))
+            return got
 
-        for tile in (spread["c"][:], spread["n"][:], words[:, T:], plane["c"][:], plane["n"][:]):
+        def move_scales(nm, got):
+            for r in range(4):
+                nc.sync.dma_start(plane[nm][r:P:32, :].bitcast(I32), got[8 * r + 4:P:32, :].bitcast(I32))
+
+        for tile in (table[:], words[:, T:], plane["c"][:], plane["n"][:]):
             nc.vector.memset(tile.bitcast(I32), 0)
-        load("c", 0, 1)
         nc.sync.dma_start(lists["c"][:], offs2)
-        nc.sync.dma_start(spread["c"][0:P:8, :].bitcast(I32), pts_scales[0].bitcast(I32))
-        nc.sync.dma_start(words[:, :T].bitcast(I32), pts_words[0].bitcast(I32))
         nc.sync.dma_start(lists["n"][:], offs)
-        nc.sync.dma_start(spread["n"][0:P:8, :].bitcast(I32), pts_scales[0].bitcast(I32))
-        load("c", 1, 2)
+        nc.sync.dma_start(table[4:P:8, :].bitcast(I32), pts_scales[0].bitcast(I32))
+        load("c", 0, 4)
+        nc.sync.dma_start(words[:, :T].bitcast(I32), pts_words[0].bitcast(I32))
+        got_c = gather_scales("c")
+        got_n = gather_scales("n")
+        move_scales("c", got_c)
         load("n", 0, 2)
+        load("n", 2, 1)
+        move_scales("n", got_n)
+        load("n", 3, 1)
+        bias_sb = sb.tile([P, F // P], F32, name="bias_sb", align_bytes=64)
+        with nc.allow_non_contiguous_dma(reason="one bias value a partition"):
+            nc.sync.dma_start(bias_sb[:], bias.rearrange("(m p) o -> p (m o)", p=P))
 
         codes = {}
         planes = {}
 
-        def quant(*parts):
-            name = "".join("%s%d" % part for part in parts)
-            n = len(parts) * P
+        def quant(name, parts):
+            n = sum(src.shape[2] for nm, m0, src in parts)
             grp = sb.tile([P, n, 4], BF16, name="grp" + name, tag="grp" + name, align_bytes=64)
-            for a, part in enumerate(parts):
-                nc.scalar.copy(grp[:, a * P:(a + 1) * P, :].rearrange("p (c i) t -> p c t i", i=4),
-                               raw[part].rearrange("p t (c i) -> p c t i", i=4))
             cd = sb.tile([P, n], U32, name="codes" + name, align_bytes=64)
             pl = sb.tile([P, n], U8, name="planes" + name, align_bytes=64)
+            c0 = 0
+            for nm, m0, src in parts:
+                w = src.shape[2]
+                nc.scalar.copy(grp[:, c0:c0 + w, :].rearrange("p (c i) t -> p c t i", i=4),
+                               src.rearrange("p t (c i) -> p c t i", i=4))
+                for a in range(w // P):
+                    codes[nm, m0 + a] = cd[:, c0 + a * P:c0 + (a + 1) * P]
+                    planes[nm, m0 + a] = pl[:, c0 + a * P:c0 + (a + 1) * P]
+                c0 = c0 + w
             nc.vector.quantize_mx(out=cd[:].bitcast(FP8X4), scales=pl[:],
                                   in_=grp[:].rearrange("p c t -> p (c t)"))
-            for a, part in enumerate(parts):
-                codes[part] = cd[:, a * P:(a + 1) * P]
-                planes[part] = pl[:, a * P:(a + 1) * P]
 
-        def gather_words(name, nm, first, count, tag):
-            if tag in at:
-                got = late.tile([P, count], U16, name=name, align_bytes=64, offset=at[tag])
+        gw = {}
+
+        def gather_words(nm, e0, halves, over):
+            name = "gw_%s%d" % (nm, e0)
+            if over is None:
+                got = sb.tile([P, halves * NB], U16, name=name, align_bytes=64)
             else:
-                got = sb.tile([P, count], U16, name=name, tag=tag, align_bytes=64)
-            nc.vector.tensor_copy(got[:], words[:].indirect(lists[nm][:, first // 16:(first + count) // 16]))
-            return [got[:, c:c + NB] for c in range(0, count, NB)]
+                got = late.tile([P, halves * NB], U16, name=name, align_bytes=64, offset=at[over])
+            nc.vector.tensor_copy(got[:], words[:].indirect(lists[nm][:, e0 * GH:(e0 + halves) * GH]))
+            for e in range(halves):
+                gw[nm, e0 + e] = got[:, e * NB:(e + 1) * NB]
 
-        gather_scales("c")
-        load("n", 2, 2)
-        load("c", 3, 1)
-        gw = {"c": gather_words("gw_c", "c", 0, E, "gw_c")}
-        quant(("c", 0))
-        gather_scales("n")
-        bias_sb = late.tile([P, F // P], F32, name="bias_sb", align_bytes=64, offset=at["bias"])
-        with nc.allow_non_contiguous_dma(reason="one bias value a partition"):
-            nc.sync.dma_start(bias_sb[:], bias.rearrange("(m p) o -> p (m o)", p=P))
-        quant(("c", 1), ("c", 2))
-        gw["n"] = gather_words("gw_n0", "n", 0, NB, "raw_c1")
-        quant(("n", 0), ("n", 1))
-        gw["n"] = gw["n"] + gather_words("gw_n1", "n", NB, NB, "n0")
-        quant(("n", 2), ("n", 3))
-        quant(("c", 3))
+        gather_words("c", 0, 2, None)
+        quant("c0", [("c", 0, raw["c0"][:, :, :2 * P])])
+        gather_words("n", 0, 1, "c0")
+        quant("n0", [("n", 0, raw["n0"][:])])
+        gather_words("n", 1, 1, "n0")
+        quant("late", [("c", 2, raw["c0"][:, :, 2 * P:]), ("n", 2, raw["n2"][:]), ("n", 3, raw["n3"][:])])
 
         banks = {}
-        reuse = {(3, 0): (1, 0), (3, 1): (0, 0)}
 
         def mm(nm, m, e):
             if nm == "c":
-                banks[m, e] = ps.tile([P, NB], F32, name="bank_%d%d" % (m, e), tag="bank_%d%d" % reuse.get((m, e), (m, e)))
+                banks[m, e] = ps.tile([P, NB], F32, name="bank_%d%d" % (m, e))
             nc.tensor.matmul_mx(out=banks[m, e][:],
                                 lhsT=codes[nm, m].bitcast(FP8X4),
                                 lhsT_scale=planes[nm, m],
-                                rhs=gw[nm][e].bitcast(FP4X4),
+                                rhs=gw[nm, e].bitcast(FP4X4),
                                 rhs_scale=plane[nm][:, e * NB:(e + 1) * NB],
                                 start=(nm == "c"), stop=(nm == "n"))
 
-        for m in range(3):
+        for nm in "cn":
             for e in (0, 1):
-                mm("c", m, e)
-        for m, e in ((1, 0), (0, 0), (1, 1), (0, 1), (2, 0), (2, 1)):
-            mm("n", m, e)
+                for m in (0, 1):
+                    mm(nm, m, e)
+        for m in (2, 3):
+            for e in (0, 1):
+                for nm in "cn":
+                    mm(nm, m, e)
 
         relu = mybir.ActivationFunctionType.Relu
         HALF = NB // 2
@@ -132,42 +139,42 @@ def tile_attend_edgeconv_kernel(tc, pts_words, pts_scales, wc, wn, bias, offs, o
             nc.vector.tensor_reduce(out=dst, in_=src.rearrange("p (g j) -> p g j", j=width),
                                     axis=mybir.AxisListType.X, op=mybir.AluOpType.max)
 
-        share = (GH, 16)
         acts, steps, pairs = [], [], []
-        for e in (0, 1):
-            act = late.tile([P, 2, HALF], F32, name="act%d" % e, align_bytes=64, offset=at["c3"] + (CH // 2, 64 - CH)[e])
+        for m in (0, 1):
+            act = sb.tile([P, 2, HALF], F32, name="act%d" % m, align_bytes=64)
             nc.scalar.activation(act[:].rearrange("p h (g j) -> p h g j", j=DEG // 2),
-                                 banks[0, e][:].rearrange("p (g h j) -> p h g j", h=2, j=DEG // 2),
-                                 relu, bias=bias_sb[:, 0:1])
+                                 banks[m, 0][:].rearrange("p (g h j) -> p h g j", h=2, j=DEG // 2),
+                                 relu, bias=bias_sb[:, m:m + 1])
             acts.append(act)
-        for e, act in enumerate(acts):
-            n = share[e] * DEG // 2
-            diff = sb.tile([P, n], F32, name="diff%d" % e, tag=("grpc3", "diff1")[e], align_bytes=64)
-            nc.gpsimd.tensor_tensor(diff[:], act[:, 1, :n], act[:, 0, :n], mybir.AluOpType.subtract)
-            step = sb.tile([P, n], F32, name="step%d" % e)
+        for m, act in enumerate(acts):
+            diff = sb.tile([P, HALF], F32, name="diff%d" % m, tag=("grplate", "diff1")[m], align_bytes=64)
+            nc.gpsimd.tensor_tensor(diff[:], act[:, 1, :], act[:, 0, :], mybir.AluOpType.subtract)
+            step = sb.tile([P, HALF], F32, name="step%d" % m)
             nc.scalar.activation(step[:], diff[:], relu)
             steps.append(step)
-        for e, act in enumerate(acts):
-            n = share[e] * DEG // 2
-            pair = sb.tile([P, n], F32, name="pair%d" % e)
-            nc.gpsimd.tensor_tensor(pair[:], act[:, 0, :n], steps[e][:], mybir.AluOpType.add)
+        for m, act in enumerate(acts):
+            pair = sb.tile([P, HALF], F32, name="pair%d" % m)
+            nc.gpsimd.tensor_tensor(pair[:], act[:, 0, :], steps[m][:], mybir.AluOpType.add)
             pairs.append(pair)
 
-        best = late.tile([P, 3 * G], F32, name="best", align_bytes=64, offset=at["c3"] + 64)
-        res = sb.tile([P, 3 * G], F32, name="res", tag="grpc3", align_bytes=64)
-        res0 = late.tile([P, G], F32, name="res0", align_bytes=64, offset=at["n0"])
-        for m in (1, 2, 3):
-            cols = slice((m - 1) * G, m * G)
+        best = [late.tile([P, G], F32, name="best%d" % m, align_bytes=64, offset=at["n3"] + m * G * 4) for m in range(4)]
+        res = [sb.tile([P, G], F32, name="res%d" % m, align_bytes=64) for m in range(4)]
+
+        def finish(m, cols):
+            nc.scalar.activation(res[m][:, cols], best[m][:, cols], relu, bias=bias_sb[:, m:m + 1])
+            nc.sync.dma_start(out[m * P:(m + 1) * P, cols], res[m][:, cols])
+
+        for m in (0, 1):
+            group_max(best[m][:, GH:], banks[m, 1][:], DEG)
+            finish(m, slice(GH, G))
+        for m in (2, 3):
             for e in (0, 1):
-                if (m, e) in reuse:
-                    mm("c", m, e)
-                    mm("n", m, e)
-                group_max(best[:, cols][:, e * GH:(e + 1) * GH], banks[m, e][:], DEG)
-            nc.scalar.activation(res[:, cols], best[:, cols], relu, bias=bias_sb[:, m:m + 1])
-            nc.sync.dma_start(out[m * P:(m + 1) * P, :], res[:, cols])
-        nc.vector.tensor_reduce(out=res0[:, GH + share[1]:],
-                                in_=acts[1][:, :, share[1] * DEG // 2:].rearrange("p h (g j) -> p g h j", j=DEG // 2),
-                                axis=mybir.AxisListType.XY, op=mybir.AluOpType.max)
-        for e in (0, 1):
-            group_max(res0[:, e * GH:e * GH + share[e]], pairs[e][:], DEG // 2)
-            nc.sync.dma_start(out[:P, e * GH:(e + 1) * GH], res0[:, e * GH:(e + 1) * GH])
+                group_max(best[m][:, e * GH:(e + 1) * GH], banks[m, e][:], DEG)
+                if m == 3:
+                    finish(m, slice(e * GH, (e + 1) * GH))
+            if m == 2:
+                finish(m, slice(0, G))
+        for m in (0, 1):
+            last = late.tile([P, GH], F32, name="last%d" % m, align_bytes=64, offset=at["n0"] + m * GH * 4)
+            group_max(last[:], pairs[m][:], DEG // 2)
+            nc.sync.dma_start(out[m * P:(m + 1) * P, :GH], last[:])

@@ -109,13 +109,15 @@ def tile_attend_edgeconv_kernel(tc, pts_words, pts_scales, wc, wn, bias, offs, o
         gather_words("n", 0, 1, "c0")
         quant("n0", [("n", 0, raw["n0"][:])])
         gather_words("n", 1, 1, "n0")
-        quant("late", [("c", 2, raw["c0"][:, :, 2 * P:]), ("n", 2, raw["n2"][:]), ("n", 3, raw["n3"][:])])
+        quant("f2", [("c", 2, raw["c0"][:, :, 2 * P:3 * P]), ("n", 2, raw["n2"][:])])
+        quant("f3", [("c", 3, raw["c0"][:, :, 3 * P:]), ("n", 3, raw["n3"][:])])
 
         banks = {}
+        reuse = {(2, 0): (1, 0), (2, 1): (0, 0)}
 
         def mm(nm, m, e):
             if nm == "c":
-                banks[m, e] = ps.tile([P, NB], F32, name="bank_%d%d" % (m, e))
+                banks[m, e] = ps.tile([P, NB], F32, name="bank_%d%d" % (m, e), tag="bank_%d%d" % reuse.get((m, e), (m, e)))
             nc.tensor.matmul_mx(out=banks[m, e][:],
                                 lhsT=codes[nm, m].bitcast(FP8X4),
                                 lhsT_scale=planes[nm, m],
@@ -123,14 +125,10 @@ def tile_attend_edgeconv_kernel(tc, pts_words, pts_scales, wc, wn, bias, offs, o
                                 rhs_scale=plane[nm][:, e * NB:(e + 1) * NB],
                                 start=(nm == "c"), stop=(nm == "n"))
 
-        for nm in "cn":
-            for e in (0, 1):
-                for m in (0, 1):
-                    mm(nm, m, e)
-        for m in (2, 3):
-            for e in (0, 1):
-                for nm in "cn":
-                    mm(nm, m, e)
+        for m, e in ((1, 0), (0, 0), (1, 1), (0, 1)):
+            mm("c", m, e)
+        for m, e in ((1, 0), (0, 0), (1, 1), (0, 1)):
+            mm("n", m, e)
 
         relu = mybir.ActivationFunctionType.Relu
         HALF = NB // 2
@@ -139,42 +137,49 @@ def tile_attend_edgeconv_kernel(tc, pts_words, pts_scales, wc, wn, bias, offs, o
             nc.vector.tensor_reduce(out=dst, in_=src.rearrange("p (g j) -> p g j", j=width),
                                     axis=mybir.AxisListType.X, op=mybir.AluOpType.max)
 
+        share = (GH, 16)
         acts, steps, pairs = [], [], []
-        for m in (0, 1):
-            act = sb.tile([P, 2, HALF], F32, name="act%d" % m, align_bytes=64)
+        for e in (0, 1):
+            act = sb.tile([P, 2, HALF], F32, name="act%d" % e, align_bytes=64)
             nc.scalar.activation(act[:].rearrange("p h (g j) -> p h g j", j=DEG // 2),
-                                 banks[m, 0][:].rearrange("p (g h j) -> p h g j", h=2, j=DEG // 2),
-                                 relu, bias=bias_sb[:, m:m + 1])
+                                 banks[0, e][:].rearrange("p (g h j) -> p h g j", h=2, j=DEG // 2),
+                                 relu, bias=bias_sb[:, 0:1])
             acts.append(act)
-        for m, act in enumerate(acts):
-            diff = sb.tile([P, HALF], F32, name="diff%d" % m, tag=("grplate", "diff1")[m], align_bytes=64)
-            nc.gpsimd.tensor_tensor(diff[:], act[:, 1, :], act[:, 0, :], mybir.AluOpType.subtract)
-            step = sb.tile([P, HALF], F32, name="step%d" % m)
+        for e, act in enumerate(acts):
+            n = share[e] * DEG // 2
+            diff = sb.tile([P, n], F32, name="diff%d" % e, tag=("grpf3", "diff1")[e], align_bytes=64)
+            nc.gpsimd.tensor_tensor(diff[:], act[:, 1, :n], act[:, 0, :n], mybir.AluOpType.subtract)
+            step = sb.tile([P, n], F32, name="step%d" % e)
             nc.scalar.activation(step[:], diff[:], relu)
             steps.append(step)
-        for m, act in enumerate(acts):
-            pair = sb.tile([P, HALF], F32, name="pair%d" % m)
-            nc.gpsimd.tensor_tensor(pair[:], act[:, 0, :], steps[m][:], mybir.AluOpType.add)
+        for e, act in enumerate(acts):
+            n = share[e] * DEG // 2
+            pair = sb.tile([P, n], F32, name="pair%d" % e)
+            nc.gpsimd.tensor_tensor(pair[:], act[:, 0, :n], steps[e][:], mybir.AluOpType.add)
             pairs.append(pair)
 
-        best = [late.tile([P, G], F32, name="best%d" % m, align_bytes=64, offset=at["n3"] + m * G * 4) for m in range(4)]
-        res = [sb.tile([P, G], F32, name="res%d" % m, align_bytes=64) for m in range(4)]
-
-        def finish(m, cols):
-            nc.scalar.activation(res[m][:, cols], best[m][:, cols], relu, bias=bias_sb[:, m:m + 1])
-            nc.sync.dma_start(out[m * P:(m + 1) * P, cols], res[m][:, cols])
-
-        for m in (0, 1):
-            group_max(best[m][:, GH:], banks[m, 1][:], DEG)
-            finish(m, slice(GH, G))
-        for m in (2, 3):
+        first = sb.tile([P, GH], F32, name="first", align_bytes=64)
+        best = late.tile([P, 3 * G], F32, name="best", align_bytes=64, offset=at["n3"])
+        res = sb.tile([P, 3 * G], F32, name="res", align_bytes=64)
+        res0 = late.tile([P, G], F32, name="res0", align_bytes=64, offset=at["n0"])
+        group_max(first[:], banks[1, 0][:], DEG)
+        for m in (1, 2, 3):
+            cols = slice((m - 1) * G, m * G)
             for e in (0, 1):
-                group_max(best[m][:, e * GH:(e + 1) * GH], banks[m, e][:], DEG)
-                if m == 3:
-                    finish(m, slice(e * GH, (e + 1) * GH))
-            if m == 2:
-                finish(m, slice(0, G))
-        for m in (0, 1):
-            last = late.tile([P, GH], F32, name="last%d" % m, align_bytes=64, offset=at["n0"] + m * GH * 4)
-            group_max(last[:], pairs[m][:], DEG // 2)
-            nc.sync.dma_start(out[m * P:(m + 1) * P, :GH], last[:])
+                if m > 1:
+                    mm("c", m, e)
+                    mm("n", m, e)
+                if (m, e) != (1, 0):
+                    group_max(best[:, cols][:, e * GH:(e + 1) * GH], banks[m, e][:], DEG)
+            if m == 1:
+                nc.scalar.activation(res[:, :GH], first[:], relu, bias=bias_sb[:, m:m + 1])
+                nc.scalar.activation(res[:, GH:G], best[:, GH:G], relu, bias=bias_sb[:, m:m + 1])
+            else:
+                nc.scalar.activation(res[:, cols], best[:, cols], relu, bias=bias_sb[:, m:m + 1])
+            nc.sync.dma_start(out[m * P:(m + 1) * P, :], res[:, cols])
+        nc.vector.tensor_reduce(out=res0[:, GH + share[1]:],
+                                in_=acts[1][:, :, share[1] * DEG // 2:].rearrange("p h (g j) -> p g h j", j=DEG // 2),
+                                axis=mybir.AxisListType.XY, op=mybir.AluOpType.max)
+        for e in (0, 1):
+            group_max(res0[:, e * GH:e * GH + share[e]], pairs[e][:], DEG // 2)
+            nc.sync.dma_start(out[:P, e * GH:(e + 1) * GH], res0[:, e * GH:(e + 1) * GH])

@@ -31,7 +31,7 @@ def tile_attend_edgeconv_kernel(tc, pts_words, pts_scales, wc, wn, bias, offs, o
         words = sb.tile([P, 2 * T], U16, name="words", align_bytes=64)
         table = sb.tile([P, T], U8, name="table", align_bytes=64)
         plane = {nm: sb.tile([P, E], U8, name="plane_" + nm, align_bytes=64) for nm in "cn"}
-        at = {"c0": 0, "n0": 4 * CH, "n3": 6 * CH}
+        at = {"c0": 0, "n0": 2 * CH, "n3": 4 * CH}
 
         raw = {}
 
@@ -59,12 +59,13 @@ def tile_attend_edgeconv_kernel(tc, pts_words, pts_scales, wc, wn, bias, offs, o
         nc.sync.dma_start(lists["c"][:], offs2)
         nc.sync.dma_start(lists["n"][:], offs)
         nc.sync.dma_start(table[4:P:8, :].bitcast(I32), pts_scales[0].bitcast(I32))
-        load("c", 0, 4)
+        load("c", 0, 2)
         nc.sync.dma_start(words[:, :T].bitcast(I32), pts_words[0].bitcast(I32))
+        load("n", 0, 2)
         got_c = gather_scales("c")
         got_n = gather_scales("n")
         move_scales("c", got_c)
-        load("n", 0, 2)
+        load("c", 2, 2)
         load("n", 2, 1)
         move_scales("n", got_n)
         load("n", 3, 1)
@@ -105,12 +106,12 @@ def tile_attend_edgeconv_kernel(tc, pts_words, pts_scales, wc, wn, bias, offs, o
                 gw[nm, e0 + e] = got[:, e * NB:(e + 1) * NB]
 
         gather_words("c", 0, 2, None)
-        quant("c0", [("c", 0, raw["c0"][:, :, :2 * P])])
+        quant("c0", [("c", 0, raw["c0"][:])])
         gather_words("n", 0, 1, "c0")
         quant("n0", [("n", 0, raw["n0"][:])])
         gather_words("n", 1, 1, "n0")
-        quant("f2", [("c", 2, raw["c0"][:, :, 2 * P:3 * P]), ("n", 2, raw["n2"][:])])
-        quant("f3", [("c", 3, raw["c0"][:, :, 3 * P:]), ("n", 3, raw["n3"][:])])
+        quant("f2", [("c", 2, raw["c2"][:, :, :P]), ("n", 2, raw["n2"][:])])
+        quant("f3", [("c", 3, raw["c2"][:, :, P:]), ("n", 3, raw["n3"][:])])
 
         banks = {}
         reuse = {(2, 0): (1, 0), (2, 1): (0, 0)}
@@ -160,7 +161,7 @@ def tile_attend_edgeconv_kernel(tc, pts_words, pts_scales, wc, wn, bias, offs, o
 
         first = sb.tile([P, GH], F32, name="first", align_bytes=64)
         best = late.tile([P, 3 * G], F32, name="best", align_bytes=64, offset=at["n3"])
-        res = sb.tile([P, 3 * G], F32, name="res", align_bytes=64)
+        res = sb.tile([P, 3 * G], F32, name="res", tag="grpf3", align_bytes=64)
         res0 = late.tile([P, G], F32, name="res0", align_bytes=64, offset=at["n0"])
         group_max(first[:], banks[1, 0][:], DEG)
         for m in (1, 2, 3):

@@ -52,13 +52,14 @@ def tile_attend_edgeconv_kernel(tc, pts_words, pts_scales, wc, wn, bias, offs, o
 
         def move_scales(nm, got):
             for r in range(4):
-                nc.sync.dma_start(plane[nm][r:P:32, :].bitcast(I32), got[8 * r + 4:P:32, :].bitcast(I32))
+                nc.sync.dma_start(plane[nm][r:P:32, :].bitcast(I32), got[96 + 2 * r:P:8, :].bitcast(I32))
 
-        for tile in (table[:], words[:, T:], plane["c"][:], plane["n"][:]):
+        for tile in (table[:96, :], words[:, T:], plane["c"][:], plane["n"][:]):
             nc.vector.memset(tile.bitcast(I32), 0)
+        nc.sync.dma_start(table[96:, :].bitcast(I32),
+                          pts_scales[0].bitcast(I32).unsqueeze(1).to_broadcast([16, 2, T // 4]))
         nc.sync.dma_start(lists["c"][:], offs2)
         nc.sync.dma_start(lists["n"][:], offs)
-        nc.sync.dma_start(table[4:P:8, :].bitcast(I32), pts_scales[0].bitcast(I32))
         load("c", 0, 2)
         nc.sync.dma_start(words[:, :T].bitcast(I32), pts_words[0].bitcast(I32))
         load("n", 0, 2)
@@ -139,7 +140,7 @@ def tile_attend_edgeconv_kernel(tc, pts_words, pts_scales, wc, wn, bias, offs, o
                                     axis=mybir.AxisListType.X, op=mybir.AluOpType.max)
 
         share = (GH, 16)
-        acts, steps, pairs = [], [], []
+        acts, steps = [], []
         for e in (0, 1):
             act = sb.tile([P, 2, HALF], F32, name="act%d" % e, align_bytes=64)
             nc.scalar.activation(act[:].rearrange("p h (g j) -> p h g j", j=DEG // 2),
@@ -153,11 +154,10 @@ def tile_attend_edgeconv_kernel(tc, pts_words, pts_scales, wc, wn, bias, offs, o
             step = sb.tile([P, n], F32, name="step%d" % e)
             nc.scalar.activation(step[:], diff[:], relu)
             steps.append(step)
+        pairs = sb.tile([P, sum(share) * DEG // 2], F32, name="pairs")
         for e, act in enumerate(acts):
             n = share[e] * DEG // 2
-            pair = sb.tile([P, n], F32, name="pair%d" % e)
-            nc.gpsimd.tensor_tensor(pair[:], act[:, 0, :n], steps[e][:], mybir.AluOpType.add)
-            pairs.append(pair)
+            nc.gpsimd.tensor_tensor(pairs[:, e * HALF:e * HALF + n], act[:, 0, :n], steps[e][:], mybir.AluOpType.add)
 
         first = sb.tile([P, GH], F32, name="first", align_bytes=64)
         best = late.tile([P, 3 * G], F32, name="best", align_bytes=64, offset=at["n3"])
@@ -181,6 +181,5 @@ def tile_attend_edgeconv_kernel(tc, pts_words, pts_scales, wc, wn, bias, offs, o
         nc.vector.tensor_reduce(out=res0[:, GH + share[1]:],
                                 in_=acts[1][:, :, share[1] * DEG // 2:].rearrange("p h (g j) -> p g h j", j=DEG // 2),
                                 axis=mybir.AxisListType.XY, op=mybir.AluOpType.max)
-        for e in (0, 1):
-            group_max(res0[:, e * GH:e * GH + share[e]], pairs[e][:], DEG // 2)
-            nc.sync.dma_start(out[:P, e * GH:(e + 1) * GH], res0[:, e * GH:(e + 1) * GH])
+        group_max(res0[:, :sum(share)], pairs[:], DEG // 2)
+        nc.sync.dma_start(out[:P, :], res0[:])

@@ -28,10 +28,10 @@ def tile_attend_edgeconv_kernel(tc, pts_words, pts_scales, wc, wn, bias, offs, o
         ps = ctx.enter_context(tc.psum_pool(name="ps", bufs=1))
 
         lists = {"c": sb.tile([P, E // 16], U16, name="l_c"), "n": sb.tile([P, E // 16], U16, name="l_n")}
-        words = sb.tile([P, 2 * T], U16, name="words", align_bytes=64)
+        words = sb.tile([P, T], U16, name="words", align_bytes=64)
         table = sb.tile([P, T], U8, name="table", align_bytes=64)
         plane = {nm: sb.tile([P, E], U8, name="plane_" + nm, align_bytes=64) for nm in "cn"}
-        at = {"c0": 0, "n0": 2 * CH, "n3": 4 * CH}
+        at = {"c0": 0, "c1": CH, "n0": 2 * CH, "n3": 4 * CH}
 
         raw = {}
 
@@ -54,14 +54,14 @@ def tile_attend_edgeconv_kernel(tc, pts_words, pts_scales, wc, wn, bias, offs, o
             for r in range(4):
                 nc.sync.dma_start(plane[nm][r:P:32, :].bitcast(I32), got[96 + 2 * r:P:8, :].bitcast(I32))
 
-        for tile in (table[:96, :], words[:, T:], plane["c"][:], plane["n"][:]):
+        for tile in (table[:96, :], plane["c"][:], plane["n"][:]):
             nc.vector.memset(tile.bitcast(I32), 0)
         nc.sync.dma_start(table[96:, :].bitcast(I32),
                           pts_scales[0].bitcast(I32).unsqueeze(1).to_broadcast([16, 2, T // 4]))
         nc.sync.dma_start(lists["c"][:], offs2)
         nc.sync.dma_start(lists["n"][:], offs)
         load("c", 0, 2)
-        nc.sync.dma_start(words[:, :T].bitcast(I32), pts_words[0].bitcast(I32))
+        nc.sync.dma_start(words[:].bitcast(I32), pts_words[0].bitcast(I32))
         load("n", 0, 2)
         got_c = gather_scales("c")
         got_n = gather_scales("n")
@@ -106,9 +106,10 @@ def tile_attend_edgeconv_kernel(tc, pts_words, pts_scales, wc, wn, bias, offs, o
             for e in range(halves):
                 gw[nm, e0 + e] = got[:, e * NB:(e + 1) * NB]
 
-        gather_words("c", 0, 2, None)
+        gather_words("c", 0, 1, None)
         quant("c0", [("c", 0, raw["c0"][:])])
-        gather_words("n", 0, 1, "c0")
+        gather_words("c", 1, 1, "c0")
+        gather_words("n", 0, 1, "c1")
         quant("n0", [("n", 0, raw["n0"][:])])
         gather_words("n", 1, 1, "n0")
         quant("f2", [("c", 2, raw["c2"][:, :, :P]), ("n", 2, raw["n2"][:])])

@@ -10,13 +10,20 @@ U16 = mybir.dt.uint16
 U8 = mybir.dt.uint8
 FP8X4 = mybir.dt.float8_e4m3fn_x4
 FP4X4 = mybir.dt.float4_e2m1fn_x4
+RELU = mybir.ActivationFunctionType.Relu
+ALU = mybir.AluOpType
+AXIS = mybir.AxisListType
 
 P = 128
 K, T, E, F, G = 512, 2048, 1024, 512, 64
+BLOCKS = K // 32
 DEG = E // G
 NB = 512
 GH = NB // DEG
-CH = 4 * P * 4
+PAIRS = NB // 2
+RAW = 4 * P * 4
+LAST_QUADRANT = 96
+SHARE = (GH, 16)
 FLOPS = 2 * 2 * K * F * E
 
 
@@ -24,163 +31,155 @@ def tile_attend_edgeconv_kernel(tc, pts_words, pts_scales, wc, wn, bias, offs, o
     nc = tc.nc
     with ExitStack() as ctx:
         sb = ctx.enter_context(tc.tile_pool(name="sb", bufs=1))
-        late = ctx.enter_context(tc.tile_pool(name="late", bufs=1))
+        placed = ctx.enter_context(tc.tile_pool(name="placed", bufs=1))
         ps = ctx.enter_context(tc.psum_pool(name="ps", bufs=1))
 
-        lists = {"c": sb.tile([P, E // 16], U16, name="l_c"), "n": sb.tile([P, E // 16], U16, name="l_n")}
+        lists = {"c": sb.tile([P, E // DEG], U16, name="list_c"), "n": sb.tile([P, E // DEG], U16, name="list_n")}
         words = sb.tile([P, T], U16, name="words", align_bytes=64)
         table = sb.tile([P, T], U8, name="table", align_bytes=64)
-        plane = {nm: sb.tile([P, E], U8, name="plane_" + nm, align_bytes=64) for nm in "cn"}
-        at = {"c0": 0, "c1": CH, "n0": 2 * CH, "n3": 4 * CH}
+        point_plane = {side: sb.tile([P, E], U8, name="plane_" + side, align_bytes=64) for side in "cn"}
+        at = {"c0": 0, "c1": RAW, "n0": 2 * RAW, "n3": 4 * RAW}
 
         raw = {}
 
-        def load(nm, m0, mt):
-            w = wc if nm == "c" else wn
-            name = "%s%d" % (nm, m0)
+        def load_weights(side, m0, tiles):
+            w = wc if side == "c" else wn
+            name = "%s%d" % (side, m0)
             if name in at:
-                tile = late.tile([P, 4, mt * P], F32, name="raw_" + name, align_bytes=64, offset=at[name])
+                tile = placed.tile([P, 4, tiles * P], F32, name="raw_" + name, align_bytes=64, offset=at[name])
             else:
-                tile = sb.tile([P, 4, mt * P], F32, name="raw_" + name, align_bytes=64)
-            nc.sync.dma_start(tile[:], w.rearrange("(p j) f -> p j f", j=4)[:, :, m0 * P:(m0 + mt) * P])
+                tile = sb.tile([P, 4, tiles * P], F32, name="raw_" + name, align_bytes=64)
+            nc.sync.dma_start(tile[:], w.rearrange("(p j) f -> p j f", j=4)[:, :, m0 * P:(m0 + tiles) * P])
             raw[name] = tile
 
-        def gather_scales(nm):
-            got = sb.tile([P, E], U8, name="got_" + nm, align_bytes=64)
-            nc.vector.tensor_copy(got[:], table[:].indirect(lists[nm][:]))
-            return got
+        def gather_scales(side):
+            picked = sb.tile([P, E], U8, name="picked_" + side, align_bytes=64)
+            nc.vector.tensor_copy(picked[:], table[:].indirect(lists[side][:]))
+            return picked
 
-        def move_scales(nm, got):
+        def move_scales(side, picked):
+            first_row = LAST_QUADRANT + "cn".index(side)
             for r in range(4):
-                nc.sync.dma_start(plane[nm][r:P:32, :].bitcast(I32), got[96 + 2 * r:P:8, :].bitcast(I32))
+                nc.sync.dma_start(point_plane[side][r:P:32, :].bitcast(I32),
+                                  picked[first_row + 2 * r:P:8, :].bitcast(I32))
 
-        for tile in (table[:96, :], plane["c"][:], plane["n"][:]):
-            nc.vector.memset(tile.bitcast(I32), 0)
-        nc.sync.dma_start(table[96:, :].bitcast(I32),
-                          pts_scales[0].bitcast(I32).unsqueeze(1).to_broadcast([16, 2, T // 4]))
+        for zeroed in (table[:LAST_QUADRANT, :], point_plane["c"][:], point_plane["n"][:]):
+            nc.vector.memset(zeroed.bitcast(I32), 0)
+        nc.sync.dma_start(table[LAST_QUADRANT:, :].bitcast(I32),
+                          pts_scales[0].bitcast(I32).unsqueeze(1).to_broadcast([BLOCKS, 2, T // 4]))
         nc.sync.dma_start(lists["c"][:], offs2)
         nc.sync.dma_start(lists["n"][:], offs)
-        load("c", 0, 2)
+        load_weights("c", 0, 2)
         nc.sync.dma_start(words[:].bitcast(I32), pts_words[0].bitcast(I32))
-        load("n", 0, 2)
-        got_c = gather_scales("c")
-        got_n = gather_scales("n")
-        move_scales("c", got_c)
-        load("c", 2, 2)
-        load("n", 2, 1)
-        move_scales("n", got_n)
-        load("n", 3, 1)
+        load_weights("n", 0, 2)
+        picked = {side: gather_scales(side) for side in "cn"}
+        move_scales("c", picked["c"])
+        load_weights("c", 2, 2)
+        load_weights("n", 2, 1)
+        move_scales("n", picked["n"])
+        load_weights("n", 3, 1)
         bias_sb = sb.tile([P, F // P], F32, name="bias_sb", align_bytes=64)
         with nc.allow_non_contiguous_dma(reason="one bias value a partition"):
             nc.sync.dma_start(bias_sb[:], bias.rearrange("(m p) o -> p (m o)", p=P))
 
         codes = {}
-        planes = {}
+        weight_plane = {}
 
-        def quant(name, parts):
-            n = sum(src.shape[2] for nm, m0, src in parts)
-            grp = sb.tile([P, n, 4], BF16, name="grp" + name, tag="grp" + name, align_bytes=64)
-            cd = sb.tile([P, n], U32, name="codes" + name, align_bytes=64)
-            pl = sb.tile([P, n], U8, name="planes" + name, align_bytes=64)
-            c0 = 0
-            for nm, m0, src in parts:
-                w = src.shape[2]
-                nc.scalar.copy(grp[:, c0:c0 + w, :].rearrange("p (c i) t -> p c t i", i=4),
+        def quantise(name, parts):
+            width = sum(src.shape[2] for side, m0, src in parts)
+            rounded = sb.tile([P, width, 4], BF16, name="rounded_" + name, tag="rounded_" + name, align_bytes=64)
+            code_tile = sb.tile([P, width], U32, name="codes_" + name, align_bytes=64)
+            plane_tile = sb.tile([P, width], U8, name="planes_" + name, align_bytes=64)
+            col = 0
+            for side, m0, src in parts:
+                part = src.shape[2]
+                nc.scalar.copy(rounded[:, col:col + part, :].rearrange("p (c i) t -> p c t i", i=4),
                                src.rearrange("p t (c i) -> p c t i", i=4))
-                for a in range(w // P):
-                    codes[nm, m0 + a] = cd[:, c0 + a * P:c0 + (a + 1) * P]
-                    planes[nm, m0 + a] = pl[:, c0 + a * P:c0 + (a + 1) * P]
-                c0 = c0 + w
-            nc.vector.quantize_mx(out=cd[:].bitcast(FP8X4), scales=pl[:],
-                                  in_=grp[:].rearrange("p c t -> p (c t)"))
+                for a in range(part // P):
+                    codes[side, m0 + a] = code_tile[:, col + a * P:col + (a + 1) * P]
+                    weight_plane[side, m0 + a] = plane_tile[:, col + a * P:col + (a + 1) * P]
+                col = col + part
+            nc.vector.quantize_mx(out=code_tile[:].bitcast(FP8X4), scales=plane_tile[:],
+                                  in_=rounded[:].rearrange("p c t -> p (c t)"))
 
-        gw = {}
+        point_words = {}
 
-        def gather_words(nm, e0, halves, over):
-            name = "gw_%s%d" % (nm, e0)
-            if over is None:
-                got = sb.tile([P, halves * NB], U16, name=name, align_bytes=64)
-            else:
-                got = late.tile([P, halves * NB], U16, name=name, align_bytes=64, offset=at[over])
-            nc.vector.tensor_copy(got[:], words[:].indirect(lists[nm][:, e0 * GH:(e0 + halves) * GH]))
-            for e in range(halves):
-                gw[nm, e0 + e] = got[:, e * NB:(e + 1) * NB]
+        def gather_words(side, e, tile):
+            nc.vector.tensor_copy(tile[:], words[:].indirect(lists[side][:, e * GH:(e + 1) * GH]))
+            point_words[side, e] = tile
 
-        gather_words("c", 0, 1, None)
-        quant("c0", [("c", 0, raw["c0"][:])])
-        gather_words("c", 1, 1, "c0")
-        gather_words("n", 0, 1, "c1")
-        quant("n0", [("n", 0, raw["n0"][:])])
-        gather_words("n", 1, 1, "n0")
-        quant("f2", [("c", 2, raw["c2"][:, :, :P]), ("n", 2, raw["n2"][:])])
-        quant("f3", [("c", 3, raw["c2"][:, :, P:]), ("n", 3, raw["n3"][:])])
+        def over(name, raw_tile):
+            return placed.tile([P, NB], U16, name=name, align_bytes=64, offset=at[raw_tile])
+
+        gather_words("c", 0, sb.tile([P, NB], U16, name="words_c0", align_bytes=64))
+        quantise("c01", [("c", 0, raw["c0"][:])])
+        gather_words("c", 1, over("words_c1", "c0"))
+        gather_words("n", 0, over("words_n0", "c1"))
+        quantise("n01", [("n", 0, raw["n0"][:])])
+        gather_words("n", 1, over("words_n1", "n0"))
+        quantise("f2", [("c", 2, raw["c2"][:, :, :P]), ("n", 2, raw["n2"][:])])
+        quantise("f3", [("c", 3, raw["c2"][:, :, P:]), ("n", 3, raw["n3"][:])])
 
         banks = {}
         reuse = {(2, 0): (1, 0), (2, 1): (0, 0)}
 
-        def mm(nm, m, e):
-            if nm == "c":
-                banks[m, e] = ps.tile([P, NB], F32, name="bank_%d%d" % (m, e), tag="bank_%d%d" % reuse.get((m, e), (m, e)))
+        def multiply(side, m, e):
+            if side == "c":
+                banks[m, e] = ps.tile([P, NB], F32, name="bank_%d%d" % (m, e),
+                                      tag="bank_%d%d" % reuse.get((m, e), (m, e)))
             nc.tensor.matmul_mx(out=banks[m, e][:],
-                                lhsT=codes[nm, m].bitcast(FP8X4),
-                                lhsT_scale=planes[nm, m],
-                                rhs=gw[nm, e].bitcast(FP4X4),
-                                rhs_scale=plane[nm][:, e * NB:(e + 1) * NB],
-                                start=(nm == "c"), stop=(nm == "n"))
+                                lhsT=codes[side, m].bitcast(FP8X4),
+                                lhsT_scale=weight_plane[side, m],
+                                rhs=point_words[side, e][:].bitcast(FP4X4),
+                                rhs_scale=point_plane[side][:, e * NB:(e + 1) * NB],
+                                start=(side == "c"), stop=(side == "n"))
 
-        for m, e in ((1, 0), (0, 0), (1, 1), (0, 1)):
-            mm("c", m, e)
-        for m, e in ((1, 0), (0, 0), (1, 1), (0, 1)):
-            mm("n", m, e)
-
-        relu = mybir.ActivationFunctionType.Relu
-        HALF = NB // 2
+        for side in "cn":
+            for e in (0, 1):
+                for m in (1, 0):
+                    multiply(side, m, e)
 
         def group_max(dst, src, width):
-            nc.vector.tensor_reduce(out=dst, in_=src.rearrange("p (g j) -> p g j", j=width),
-                                    axis=mybir.AxisListType.X, op=mybir.AluOpType.max)
+            nc.vector.tensor_reduce(out=dst, in_=src.rearrange("p (g j) -> p g j", j=width), axis=AXIS.X, op=ALU.max)
 
-        share = (GH, 16)
-        acts, steps = [], []
+        actives, steps = [], []
         for e in (0, 1):
-            act = sb.tile([P, 2, HALF], F32, name="act%d" % e, align_bytes=64)
-            nc.scalar.activation(act[:].rearrange("p h (g j) -> p h g j", j=DEG // 2),
+            active = sb.tile([P, 2, PAIRS], F32, name="active%d" % e, align_bytes=64)
+            nc.scalar.activation(active[:].rearrange("p h (g j) -> p h g j", j=DEG // 2),
                                  banks[0, e][:].rearrange("p (g h j) -> p h g j", h=2, j=DEG // 2),
-                                 relu, bias=bias_sb[:, 0:1])
-            acts.append(act)
-        for e, act in enumerate(acts):
-            n = share[e] * DEG // 2
-            diff = sb.tile([P, n], F32, name="diff%d" % e, tag=("grpf3", "diff1")[e], align_bytes=64)
-            nc.gpsimd.tensor_tensor(diff[:], act[:, 1, :n], act[:, 0, :n], mybir.AluOpType.subtract)
+                                 RELU, bias=bias_sb[:, 0:1])
+            actives.append(active)
+        for e, active in enumerate(actives):
+            n = SHARE[e] * DEG // 2
+            diff = sb.tile([P, n], F32, name="diff%d" % e, tag=("rounded_f3", "diff1")[e], align_bytes=64)
+            nc.gpsimd.tensor_tensor(diff[:], active[:, 1, :n], active[:, 0, :n], ALU.subtract)
             step = sb.tile([P, n], F32, name="step%d" % e)
-            nc.scalar.activation(step[:], diff[:], relu)
+            nc.scalar.activation(step[:], diff[:], RELU)
             steps.append(step)
-        pairs = sb.tile([P, sum(share) * DEG // 2], F32, name="pairs")
-        for e, act in enumerate(acts):
-            n = share[e] * DEG // 2
-            nc.gpsimd.tensor_tensor(pairs[:, e * HALF:e * HALF + n], act[:, 0, :n], steps[e][:], mybir.AluOpType.add)
+        pair_max = sb.tile([P, sum(SHARE) * DEG // 2], F32, name="pair_max")
+        for e, active in enumerate(actives):
+            n = SHARE[e] * DEG // 2
+            nc.gpsimd.tensor_tensor(pair_max[:, e * PAIRS:e * PAIRS + n], active[:, 0, :n], steps[e][:], ALU.add)
 
-        first = sb.tile([P, GH], F32, name="first", align_bytes=64)
-        best = late.tile([P, 3 * G], F32, name="best", align_bytes=64, offset=at["n3"])
-        res = sb.tile([P, 3 * G], F32, name="res", tag="grpf3", align_bytes=64)
-        res0 = late.tile([P, G], F32, name="res0", align_bytes=64, offset=at["n0"])
-        group_max(first[:], banks[1, 0][:], DEG)
-        for m in (1, 2, 3):
+        best_first = sb.tile([P, GH], F32, name="best_first", align_bytes=64)
+        best = placed.tile([P, 3 * G], F32, name="best", align_bytes=64, offset=at["n3"])
+        result = sb.tile([P, 3 * G], F32, name="result", tag="rounded_f3", align_bytes=64)
+        result0 = placed.tile([P, G], F32, name="result0", align_bytes=64, offset=at["n0"])
+
+        group_max(best_first[:], banks[1, 0][:], DEG)
+        group_max(best[:, GH:G], banks[1, 1][:], DEG)
+        nc.scalar.activation(result[:, :GH], best_first[:], RELU, bias=bias_sb[:, 1:2])
+        nc.scalar.activation(result[:, GH:G], best[:, GH:G], RELU, bias=bias_sb[:, 1:2])
+        nc.sync.dma_start(out[P:2 * P, :], result[:, :G])
+        for m in (2, 3):
             cols = slice((m - 1) * G, m * G)
             for e in (0, 1):
-                if m > 1:
-                    mm("c", m, e)
-                    mm("n", m, e)
-                if (m, e) != (1, 0):
-                    group_max(best[:, cols][:, e * GH:(e + 1) * GH], banks[m, e][:], DEG)
-            if m == 1:
-                nc.scalar.activation(res[:, :GH], first[:], relu, bias=bias_sb[:, m:m + 1])
-                nc.scalar.activation(res[:, GH:G], best[:, GH:G], relu, bias=bias_sb[:, m:m + 1])
-            else:
-                nc.scalar.activation(res[:, cols], best[:, cols], relu, bias=bias_sb[:, m:m + 1])
-            nc.sync.dma_start(out[m * P:(m + 1) * P, :], res[:, cols])
-        nc.vector.tensor_reduce(out=res0[:, GH + share[1]:],
-                                in_=acts[1][:, :, share[1] * DEG // 2:].rearrange("p h (g j) -> p g h j", j=DEG // 2),
-                                axis=mybir.AxisListType.XY, op=mybir.AluOpType.max)
-        group_max(res0[:, :sum(share)], pairs[:], DEG // 2)
-        nc.sync.dma_start(out[:P, :], res0[:])
+                multiply("c", m, e)
+                multiply("n", m, e)
+                group_max(best[:, cols][:, e * GH:(e + 1) * GH], banks[m, e][:], DEG)
+            nc.scalar.activation(result[:, cols], best[:, cols], RELU, bias=bias_sb[:, m:m + 1])
+            nc.sync.dma_start(out[m * P:(m + 1) * P, :], result[:, cols])
+        rest = actives[1][:, :, SHARE[1] * DEG // 2:].rearrange("p h (g j) -> p g h j", j=DEG // 2)
+        nc.vector.tensor_reduce(out=result0[:, sum(SHARE):], in_=rest, axis=AXIS.XY, op=ALU.max)
+        group_max(result0[:, :sum(SHARE)], pair_max[:], DEG // 2)
+        nc.sync.dma_start(out[:P, :], result0[:])

@@ -121,18 +121,17 @@ def tile_attend_edgeconv_kernel(tc, pts_words, pts_scales, wc, wn, bias, offs, o
         quantise("f3", [("c", 3, raw["c2"][:, :, P:]), ("n", 3, raw["n3"][:])])
 
         banks = {}
-        reuse = {(2, 0): (1, 0), (2, 1): (0, 0)}
 
         def multiply(side, m, e):
-            if side == "c":
-                banks[m, e] = ps.tile([P, NB], F32, name="bank_%d%d" % (m, e),
-                                      tag="bank_%d%d" % reuse.get((m, e), (m, e)))
+            opens = (m, e) not in banks
+            if opens:
+                banks[m, e] = ps.tile([P, NB], F32, name="bank_%d%d" % (m, e))
             nc.tensor.matmul_mx(out=banks[m, e][:],
                                 lhsT=codes[side, m].bitcast(FP8X4),
                                 lhsT_scale=weight_plane[side, m],
                                 rhs=point_words[side, e][:].bitcast(FP4X4),
                                 rhs_scale=point_plane[side][:, e * NB:(e + 1) * NB],
-                                start=(side == "c"), stop=(side == "n"))
+                                start=opens, stop=not opens)
 
         for side in "cn":
             for e in (0, 1):
@@ -174,8 +173,8 @@ def tile_attend_edgeconv_kernel(tc, pts_words, pts_scales, wc, wn, bias, offs, o
         for m in (2, 3):
             cols = slice((m - 1) * G, m * G)
             for e in (0, 1):
-                multiply("c", m, e)
                 multiply("n", m, e)
+                multiply("c", m, e)
                 group_max(best[:, cols][:, e * GH:(e + 1) * GH], banks[m, e][:], DEG)
             nc.scalar.activation(result[:, cols], best[:, cols], RELU, bias=bias_sb[:, m:m + 1])
             nc.sync.dma_start(out[m * P:(m + 1) * P, :], result[:, cols])

@@ -38,7 +38,7 @@ def tile_attend_edgeconv_kernel(tc, pts_words, pts_scales, wc, wn, bias, offs, o
         words = sb.tile([P, T], U16, name="words", align_bytes=64)
         table = sb.tile([P, T], U8, name="table", align_bytes=64)
         point_plane = {side: sb.tile([P, E], U8, name="plane_" + side, align_bytes=64) for side in "cn"}
-        at = {"c0": 0, "c1": RAW, "n0": 2 * RAW, "n3": 4 * RAW}
+        at = {"c0": 0, "c1": RAW, "n2": 2 * RAW, "n3": 3 * RAW}
 
         raw = {}
 
@@ -74,8 +74,8 @@ def tile_attend_edgeconv_kernel(tc, pts_words, pts_scales, wc, wn, bias, offs, o
         load_weights("n", 0, 2)
         picked = {side: gather_scales(side) for side in "cn"}
         move_scales("c", picked["c"])
-        load_weights("c", 2, 2)
         load_weights("n", 2, 1)
+        load_weights("c", 2, 2)
         move_scales("n", picked["n"])
         load_weights("n", 3, 1)
         bias_sb = sb.tile([P, F // P], F32, name="bias_sb", align_bytes=64)
@@ -115,10 +115,10 @@ def tile_attend_edgeconv_kernel(tc, pts_words, pts_scales, wc, wn, bias, offs, o
         quantise("c01", [("c", 0, raw["c0"][:])])
         gather_words("c", 1, over("words_c1", "c0"))
         gather_words("n", 0, over("words_n0", "c1"))
-        quantise("n01", [("n", 0, raw["n0"][:])])
-        gather_words("n", 1, over("words_n1", "n0"))
-        quantise("f2", [("c", 2, raw["c2"][:, :, :P]), ("n", 2, raw["n2"][:])])
-        quantise("f3", [("c", 3, raw["c2"][:, :, P:]), ("n", 3, raw["n3"][:])])
+        quantise("n012", [("n", 0, raw["n0"][:]), ("n", 2, raw["n2"][:])])
+        gather_words("n", 1, over("words_n1", "n2"))
+        quantise("c23", [("c", 2, raw["c2"][:])])
+        quantise("n3", [("n", 3, raw["n3"][:])])
 
         banks = {}
 
@@ -137,48 +137,54 @@ def tile_attend_edgeconv_kernel(tc, pts_words, pts_scales, wc, wn, bias, offs, o
             for e in (0, 1):
                 for m in (1, 0):
                     multiply(side, m, e)
+                if (side, e) == ("n", 0):
+                    multiply("n", 2, 0)
 
         def group_max(dst, src, width):
             nc.vector.tensor_reduce(out=dst, in_=src.rearrange("p (g j) -> p g j", j=width), axis=AXIS.X, op=ALU.max)
 
         actives, steps = [], []
         for e in (0, 1):
-            active = sb.tile([P, 2, PAIRS], F32, name="active%d" % e, align_bytes=64)
+            active = sb.tile([P, 2, SHARE[e] * DEG // 2], F32, name="active%d" % e, align_bytes=64)
             nc.scalar.activation(active[:].rearrange("p h (g j) -> p h g j", j=DEG // 2),
-                                 banks[0, e][:].rearrange("p (g h j) -> p h g j", h=2, j=DEG // 2),
+                                 banks[0, e][:, :SHARE[e] * DEG].rearrange("p (g h j) -> p h g j", h=2, j=DEG // 2),
                                  RELU, bias=bias_sb[:, 0:1])
             actives.append(active)
+        rest = sb.tile([P, NB - SHARE[1] * DEG], F32, name="rest", align_bytes=64)
+        nc.scalar.activation(rest[:], banks[0, 1][:, SHARE[1] * DEG:], RELU, bias=bias_sb[:, 0:1])
         for e, active in enumerate(actives):
             n = SHARE[e] * DEG // 2
-            diff = sb.tile([P, n], F32, name="diff%d" % e, tag=("rounded_f3", "diff1")[e], align_bytes=64)
-            nc.gpsimd.tensor_tensor(diff[:], active[:, 1, :n], active[:, 0, :n], ALU.subtract)
+            diff = sb.tile([P, n], F32, name="diff%d" % e, tag=("rounded_n3", "diff1")[e], align_bytes=64)
+            nc.gpsimd.tensor_tensor(diff[:], active[:, 1, :], active[:, 0, :], ALU.subtract)
             step = sb.tile([P, n], F32, name="step%d" % e)
             nc.scalar.activation(step[:], diff[:], RELU)
             steps.append(step)
         pair_max = sb.tile([P, sum(SHARE) * DEG // 2], F32, name="pair_max")
         for e, active in enumerate(actives):
             n = SHARE[e] * DEG // 2
-            nc.gpsimd.tensor_tensor(pair_max[:, e * PAIRS:e * PAIRS + n], active[:, 0, :n], steps[e][:], ALU.add)
+            nc.gpsimd.tensor_tensor(pair_max[:, e * PAIRS:e * PAIRS + n], active[:, 0, :], steps[e][:], ALU.add)
 
         best_first = sb.tile([P, GH], F32, name="best_first", align_bytes=64)
         best = placed.tile([P, 3 * G], F32, name="best", align_bytes=64, offset=at["n3"])
-        result = sb.tile([P, 3 * G], F32, name="result", tag="rounded_f3", align_bytes=64)
-        result0 = placed.tile([P, G], F32, name="result0", align_bytes=64, offset=at["n0"])
+        result = sb.tile([P, 3 * G], F32, name="result", tag="rounded_n3", align_bytes=64)
+        result0 = placed.tile([P, G], F32, name="result0", align_bytes=64, offset=at["n2"])
 
         group_max(best_first[:], banks[1, 0][:], DEG)
         group_max(best[:, GH:G], banks[1, 1][:], DEG)
         nc.scalar.activation(result[:, :GH], best_first[:], RELU, bias=bias_sb[:, 1:2])
+        nc.sync.dma_start(out[P:2 * P, :GH], result[:, :GH])
         nc.scalar.activation(result[:, GH:G], best[:, GH:G], RELU, bias=bias_sb[:, 1:2])
-        nc.sync.dma_start(out[P:2 * P, :], result[:, :G])
+        nc.sync.dma_start(out[P:2 * P, GH:], result[:, GH:G])
         for m in (2, 3):
             cols = slice((m - 1) * G, m * G)
             for e in (0, 1):
-                multiply("n", m, e)
+                if (m, e) != (2, 0):
+                    multiply("n", m, e)
                 multiply("c", m, e)
                 group_max(best[:, cols][:, e * GH:(e + 1) * GH], banks[m, e][:], DEG)
             nc.scalar.activation(result[:, cols], best[:, cols], RELU, bias=bias_sb[:, m:m + 1])
             nc.sync.dma_start(out[m * P:(m + 1) * P, :], result[:, cols])
-        rest = actives[1][:, :, SHARE[1] * DEG // 2:].rearrange("p h (g j) -> p g h j", j=DEG // 2)
-        nc.vector.tensor_reduce(out=result0[:, sum(SHARE):], in_=rest, axis=AXIS.XY, op=ALU.max)
+        group_max(result0[:, sum(SHARE):], rest[:], DEG)
+        nc.sync.dma_start(out[:P, sum(SHARE):], result0[:, sum(SHARE):])
         group_max(result0[:, :sum(SHARE)], pair_max[:], DEG // 2)
-        nc.sync.dma_start(out[:P, :], result0[:])
+        nc.sync.dma_start(out[:P, :sum(SHARE)], result0[:, :sum(SHARE)])

@@ -78,9 +78,11 @@ def tile_attend_edgeconv_kernel(tc, pts_words, pts_scales, wc, wn, bias, offs, o
         load_weights("c", 2, 2)
         move_scales("n", picked["n"])
         load_weights("n", 3, 1)
-        bias_sb = sb.tile([P, F // P], F32, name="bias_sb", align_bytes=64)
+        bias0 = sb.tile([P, 1], F32, name="bias0", align_bytes=64)
+        bias123 = sb.tile([P, 3], F32, name="bias123", align_bytes=64)
         with nc.allow_non_contiguous_dma(reason="one bias value a partition"):
-            nc.sync.dma_start(bias_sb[:], bias.rearrange("(m p) o -> p (m o)", p=P))
+            nc.sync.dma_start(bias0[:], bias[:P, :])
+            nc.sync.dma_start(bias123[:], bias[P:, :].rearrange("(m p) o -> p (m o)", p=P))
 
         codes = {}
         weight_plane = {}
@@ -148,10 +150,10 @@ def tile_attend_edgeconv_kernel(tc, pts_words, pts_scales, wc, wn, bias, offs, o
             active = sb.tile([P, 2, SHARE[e] * DEG // 2], F32, name="active%d" % e, align_bytes=64)
             nc.scalar.activation(active[:].rearrange("p h (g j) -> p h g j", j=DEG // 2),
                                  banks[0, e][:, :SHARE[e] * DEG].rearrange("p (g h j) -> p h g j", h=2, j=DEG // 2),
-                                 RELU, bias=bias_sb[:, 0:1])
+                                 RELU, bias=bias0[:])
             actives.append(active)
         rest = sb.tile([P, NB - SHARE[1] * DEG], F32, name="rest", align_bytes=64)
-        nc.scalar.activation(rest[:], banks[0, 1][:, SHARE[1] * DEG:], RELU, bias=bias_sb[:, 0:1])
+        nc.scalar.activation(rest[:], banks[0, 1][:, SHARE[1] * DEG:], RELU, bias=bias0[:])
         for e, active in enumerate(actives):
             n = SHARE[e] * DEG // 2
             diff = sb.tile([P, n], F32, name="diff%d" % e, tag=("rounded_n3", "diff1")[e], align_bytes=64)
@@ -171,9 +173,9 @@ def tile_attend_edgeconv_kernel(tc, pts_words, pts_scales, wc, wn, bias, offs, o
 
         group_max(best_first[:], banks[1, 0][:], DEG)
         group_max(best[:, GH:G], banks[1, 1][:], DEG)
-        nc.scalar.activation(result[:, :GH], best_first[:], RELU, bias=bias_sb[:, 1:2])
+        nc.scalar.activation(result[:, :GH], best_first[:], RELU, bias=bias123[:, 0:1])
         nc.sync.dma_start(out[P:2 * P, :GH], result[:, :GH])
-        nc.scalar.activation(result[:, GH:G], best[:, GH:G], RELU, bias=bias_sb[:, 1:2])
+        nc.scalar.activation(result[:, GH:G], best[:, GH:G], RELU, bias=bias123[:, 0:1])
         nc.sync.dma_start(out[P:2 * P, GH:], result[:, GH:G])
         for m in (2, 3):
             cols = slice((m - 1) * G, m * G)
@@ -182,9 +184,8 @@ def tile_attend_edgeconv_kernel(tc, pts_words, pts_scales, wc, wn, bias, offs, o
                     multiply("n", m, e)
                 multiply("c", m, e)
                 group_max(best[:, cols][:, e * GH:(e + 1) * GH], banks[m, e][:], DEG)
-            nc.scalar.activation(result[:, cols], best[:, cols], RELU, bias=bias_sb[:, m:m + 1])
+            nc.scalar.activation(result[:, cols], best[:, cols], RELU, bias=bias123[:, m - 1:m])
             nc.sync.dma_start(out[m * P:(m + 1) * P, :], result[:, cols])
         group_max(result0[:, sum(SHARE):], rest[:], DEG)
-        nc.sync.dma_start(out[:P, sum(SHARE):], result0[:, sum(SHARE):])
         group_max(result0[:, :sum(SHARE)], pair_max[:], DEG // 2)
-        nc.sync.dma_start(out[:P, :sum(SHARE)], result0[:, :sum(SHARE)])
+        nc.sync.dma_start(out[:P, :], result0[:])

@@ -20,10 +20,9 @@ BLOCKS = K // 32
 DEG = E // G
 NB = 512
 GH = NB // DEG
-PAIRS = NB // 2
 RAW = 4 * P * 4
 LAST_QUADRANT = 96
-SHARE = (GH, 16)
+PIECE = 24
 FLOPS = 2 * 2 * K * F * E
 
 
@@ -145,26 +144,30 @@ def tile_attend_edgeconv_kernel(tc, pts_words, pts_scales, wc, wn, bias, offs, o
         def group_max(dst, src, width):
             nc.vector.tensor_reduce(out=dst, in_=src.rearrange("p (g j) -> p g j", j=width), axis=AXIS.X, op=ALU.max)
 
-        actives, steps = [], []
-        for e in (0, 1):
-            active = sb.tile([P, 2, SHARE[e] * DEG // 2], F32, name="active%d" % e, align_bytes=64)
-            nc.scalar.activation(active[:].rearrange("p h (g j) -> p h g j", j=DEG // 2),
-                                 banks[0, e][:, :SHARE[e] * DEG].rearrange("p (g h j) -> p h g j", h=2, j=DEG // 2),
+        def activate_pairs(active, at_centre, e, g0, g1):
+            cols = slice(at_centre * DEG // 2, (at_centre + g1 - g0) * DEG // 2)
+            nc.scalar.activation(active[:, :, cols].rearrange("p h (g j) -> p h g j", j=DEG // 2),
+                                 banks[0, e][:, g0 * DEG:g1 * DEG].rearrange("p (g h j) -> p h g j", h=2, j=DEG // 2),
                                  RELU, bias=bias0[:])
-            actives.append(active)
-        rest = sb.tile([P, NB - SHARE[1] * DEG], F32, name="rest", align_bytes=64)
-        nc.scalar.activation(rest[:], banks[0, 1][:, SHARE[1] * DEG:], RELU, bias=bias0[:])
-        for e, active in enumerate(actives):
-            n = SHARE[e] * DEG // 2
-            diff = sb.tile([P, n], F32, name="diff%d" % e, tag=("rounded_n3", "diff1")[e], align_bytes=64)
+
+        n = PIECE * DEG // 2
+        late = 2 * PIECE - GH
+        actives = [sb.tile([P, 2, n], F32, name="active%d" % piece, align_bytes=64) for piece in (0, 1)]
+        activate_pairs(actives[0], 0, 0, 0, PIECE)
+        activate_pairs(actives[1], 0, 0, PIECE, GH)
+        activate_pairs(actives[1], GH - PIECE, 1, 0, late)
+        rest = sb.tile([P, NB - late * DEG], F32, name="rest", align_bytes=64)
+        nc.scalar.activation(rest[:], banks[0, 1][:, late * DEG:], RELU, bias=bias0[:])
+        steps = []
+        for piece, active in enumerate(actives):
+            diff = sb.tile([P, n], F32, name="diff%d" % piece, tag=("rounded_n3", "diff1")[piece], align_bytes=64)
             nc.gpsimd.tensor_tensor(diff[:], active[:, 1, :], active[:, 0, :], ALU.subtract)
-            step = sb.tile([P, n], F32, name="step%d" % e)
+            step = sb.tile([P, n], F32, name="step%d" % piece)
             nc.scalar.activation(step[:], diff[:], RELU)
             steps.append(step)
-        pair_max = sb.tile([P, sum(SHARE) * DEG // 2], F32, name="pair_max")
-        for e, active in enumerate(actives):
-            n = SHARE[e] * DEG // 2
-            nc.gpsimd.tensor_tensor(pair_max[:, e * PAIRS:e * PAIRS + n], active[:, 0, :], steps[e][:], ALU.add)
+        pair_max = sb.tile([P, 2 * n], F32, name="pair_max")
+        for piece, active in enumerate(actives):
+            nc.gpsimd.tensor_tensor(pair_max[:, piece * n:(piece + 1) * n], active[:, 0, :], steps[piece][:], ALU.add)
 
         best_first = sb.tile([P, GH], F32, name="best_first", align_bytes=64)
         best = placed.tile([P, 3 * G], F32, name="best", align_bytes=64, offset=at["n3"])
@@ -186,6 +189,6 @@ def tile_attend_edgeconv_kernel(tc, pts_words, pts_scales, wc, wn, bias, offs, o
                 group_max(best[:, cols][:, e * GH:(e + 1) * GH], banks[m, e][:], DEG)
             nc.scalar.activation(result[:, cols], best[:, cols], RELU, bias=bias123[:, m - 1:m])
             nc.sync.dma_start(out[m * P:(m + 1) * P, :], result[:, cols])
-        group_max(result0[:, sum(SHARE):], rest[:], DEG)
-        group_max(result0[:, :sum(SHARE)], pair_max[:], DEG // 2)
+        group_max(result0[:, 2 * PIECE:], rest[:], DEG)
+        group_max(result0[:, :2 * PIECE], pair_max[:], DEG // 2)
         nc.sync.dma_start(out[:P, :], result0[:])

@@ -165,9 +165,9 @@ def tile_attend_edgeconv_kernel(tc, pts_words, pts_scales, wc, wn, bias, offs, o
             step = sb.tile([P, n], F32, name="step%d" % piece)
             nc.scalar.activation(step[:], diff[:], RELU)
             steps.append(step)
-        pair_max = sb.tile([P, 2 * n], F32, name="pair_max")
+        pair_max = [sb.tile([P, n], F32, name="pair_max%d" % piece) for piece in (0, 1)]
         for piece, active in enumerate(actives):
-            nc.gpsimd.tensor_tensor(pair_max[:, piece * n:(piece + 1) * n], active[:, 0, :], steps[piece][:], ALU.add)
+            nc.gpsimd.tensor_tensor(pair_max[piece][:], active[:, 0, :], steps[piece][:], ALU.add)
 
         best_first = sb.tile([P, GH], F32, name="best_first", align_bytes=64)
         best = placed.tile([P, 3 * G], F32, name="best", align_bytes=64, offset=at["n3"])
@@ -190,5 +190,6 @@ def tile_attend_edgeconv_kernel(tc, pts_words, pts_scales, wc, wn, bias, offs, o
             nc.scalar.activation(result[:, cols], best[:, cols], RELU, bias=bias123[:, m - 1:m])
             nc.sync.dma_start(out[m * P:(m + 1) * P, :], result[:, cols])
         group_max(result0[:, 2 * PIECE:], rest[:], DEG)
-        group_max(result0[:, :2 * PIECE], pair_max[:], DEG // 2)
+        for piece in (0, 1):
+            group_max(result0[:, piece * PIECE:(piece + 1) * PIECE], pair_max[piece][:], DEG // 2)
         nc.sync.dma_start(out[:P, :], result0[:])

from contextlib import ExitStack

import concourse.mybir as mybir

F32 = mybir.dt.float32
BF16 = mybir.dt.bfloat16
I32 = mybir.dt.int32
U32 = mybir.dt.uint32
U16 = mybir.dt.uint16
U8 = mybir.dt.uint8
FP8X4 = mybir.dt.float8_e4m3fn_x4
FP4X4 = mybir.dt.float4_e2m1fn_x4
RELU = mybir.ActivationFunctionType.Relu
ALU = mybir.AluOpType
AXIS = mybir.AxisListType

P = 128
K, T, E, F, G = 512, 2048, 1024, 512, 64
BLOCKS = K // 32
DEG = E // G
NB = 512
GH = NB // DEG
RAW = 4 * P * 4
LAST_QUADRANT = 96
PIECE = 24
FLOPS = 2 * 2 * K * F * E


def tile_attend_edgeconv_kernel(tc, pts_words, pts_scales, wc, wn, bias, offs, offs2, out):
    nc = tc.nc
    with ExitStack() as ctx:
        sb = ctx.enter_context(tc.tile_pool(name="sb", bufs=1))
        placed = ctx.enter_context(tc.tile_pool(name="placed", bufs=1))
        ps = ctx.enter_context(tc.psum_pool(name="ps", bufs=1))

        lists = {"c": sb.tile([P, E // DEG], U16, name="list_c"), "n": sb.tile([P, E // DEG], U16, name="list_n")}
        words = sb.tile([P, T], U16, name="words", align_bytes=64)
        table = sb.tile([P, T], U8, name="table", align_bytes=64)
        point_plane = {side: sb.tile([P, E], U8, name="plane_" + side, align_bytes=64) for side in "cn"}
        at = {"c0": 0, "c1": RAW, "n2": 2 * RAW, "n3": 3 * RAW}

        raw = {}

        def load_weights(side, m0, tiles):
            w = wc if side == "c" else wn
            name = "%s%d" % (side, m0)
            if name in at:
                tile = placed.tile([P, 4, tiles * P], F32, name="raw_" + name, align_bytes=64, offset=at[name])
            else:
                tile = sb.tile([P, 4, tiles * P], F32, name="raw_" + name, align_bytes=64)
            nc.sync.dma_start(tile[:], w.rearrange("(p j) f -> p j f", j=4)[:, :, m0 * P:(m0 + tiles) * P])
            raw[name] = tile

        def gather_scales(side):
            picked = sb.tile([P, E], U8, name="picked_" + side, align_bytes=64)
            nc.vector.tensor_copy(picked[:], table[:].indirect(lists[side][:]))
            return picked

        def move_scales(side, picked):
            first_row = LAST_QUADRANT + "cn".index(side)
            for r in range(4):
                nc.sync.dma_start(point_plane[side][r:P:32, :].bitcast(I32),
                                  picked[first_row + 2 * r:P:8, :].bitcast(I32))

        for zeroed in (table[:LAST_QUADRANT, :], point_plane["c"][:], point_plane["n"][:]):
            nc.vector.memset(zeroed.bitcast(I32), 0)
        nc.sync.dma_start(table[LAST_QUADRANT:, :].bitcast(I32),
                          pts_scales[0].bitcast(I32).unsqueeze(1).to_broadcast([BLOCKS, 2, T // 4]))
        nc.sync.dma_start(lists["c"][:], offs2)
        nc.sync.dma_start(lists["n"][:], offs)
        load_weights("c", 0, 2)
        nc.sync.dma_start(words[:].bitcast(I32), pts_words[0].bitcast(I32))
        load_weights("n", 0, 2)
        picked = {side: gather_scales(side) for side in "cn"}
        move_scales("c", picked["c"])
        load_weights("n", 2, 1)
        load_weights("c", 2, 2)
        move_scales("n", picked["n"])
        load_weights("n", 3, 1)
        bias0 = sb.tile([P, 1], F32, name="bias0", align_bytes=64)
        bias123 = sb.tile([P, 3], F32, name="bias123", align_bytes=64)
        with nc.allow_non_contiguous_dma(reason="one bias value a partition"):
            nc.sync.dma_start(bias0[:], bias[:P, :])
            nc.sync.dma_start(bias123[:], bias[P:, :].rearrange("(m p) o -> p (m o)", p=P))

        codes = {}
        weight_plane = {}

        def quantise(name, parts):
            width = sum(src.shape[2] for side, m0, src in parts)
            rounded = sb.tile([P, width, 4], BF16, name="rounded_" + name, tag="rounded_" + name, align_bytes=64)
            code_tile = sb.tile([P, width], U32, name="codes_" + name, align_bytes=64)
            plane_tile = sb.tile([P, width], U8, name="planes_" + name, align_bytes=64)
            col = 0
            for side, m0, src in parts:
                part = src.shape[2]
                nc.scalar.copy(rounded[:, col:col + part, :].rearrange("p (c i) t -> p c t i", i=4),
                               src.rearrange("p t (c i) -> p c t i", i=4))
                for a in range(part // P):
                    codes[side, m0 + a] = code_tile[:, col + a * P:col + (a + 1) * P]
                    weight_plane[side, m0 + a] = plane_tile[:, col + a * P:col + (a + 1) * P]
                col = col + part
            nc.vector.quantize_mx(out=code_tile[:].bitcast(FP8X4), scales=plane_tile[:],
                                  in_=rounded[:].rearrange("p c t -> p (c t)"))

        point_words = {}

        def gather_words(side, e, tile):
            nc.vector.tensor_copy(tile[:], words[:].indirect(lists[side][:, e * GH:(e + 1) * GH]))
            point_words[side, e] = tile

        def over(name, raw_tile):
            return placed.tile([P, NB], U16, name=name, align_bytes=64, offset=at[raw_tile])

        gather_words("c", 0, sb.tile([P, NB], U16, name="words_c0", align_bytes=64))
        quantise("c01", [("c", 0, raw["c0"][:])])
        gather_words("c", 1, over("words_c1", "c0"))
        gather_words("n", 0, over("words_n0", "c1"))
        quantise("n012", [("n", 0, raw["n0"][:]), ("n", 2, raw["n2"][:])])
        gather_words("n", 1, over("words_n1", "n2"))
        quantise("c23", [("c", 2, raw["c2"][:])])
        quantise("n3", [("n", 3, raw["n3"][:])])

        banks = {}

        def multiply(side, m, e):
            opens = (m, e) not in banks
            if opens:
                banks[m, e] = ps.tile([P, NB], F32, name="bank_%d%d" % (m, e))
            nc.tensor.matmul_mx(out=banks[m, e][:],
                                lhsT=codes[side, m].bitcast(FP8X4),
                                lhsT_scale=weight_plane[side, m],
                                rhs=point_words[side, e][:].bitcast(FP4X4),
                                rhs_scale=point_plane[side][:, e * NB:(e + 1) * NB],
                                start=opens, stop=not opens)

        for side in "cn":
            for e in (0, 1):
                for m in (1, 0):
                    multiply(side, m, e)
                if (side, e) == ("n", 0):
                    multiply("n", 2, 0)

        def group_max(dst, src, width):
            nc.vector.tensor_reduce(out=dst, in_=src.rearrange("p (g j) -> p g j", j=width), axis=AXIS.X, op=ALU.max)

        def activate_pairs(active, at_centre, e, g0, g1):
            cols = slice(at_centre * DEG // 2, (at_centre + g1 - g0) * DEG // 2)
            nc.scalar.activation(active[:, :, cols].rearrange("p h (g j) -> p h g j", j=DEG // 2),
                                 banks[0, e][:, g0 * DEG:g1 * DEG].rearrange("p (g h j) -> p h g j", h=2, j=DEG // 2),
                                 RELU, bias=bias0[:])

        n = PIECE * DEG // 2
        late = 2 * PIECE - GH
        actives = [sb.tile([P, 2, n], F32, name="active%d" % piece, align_bytes=64) for piece in (0, 1)]
        activate_pairs(actives[0], 0, 0, 0, PIECE)
        activate_pairs(actives[1], 0, 0, PIECE, GH)
        activate_pairs(actives[1], GH - PIECE, 1, 0, late)
        rest = sb.tile([P, NB - late * DEG], F32, name="rest", align_bytes=64)
        nc.scalar.activation(rest[:], banks[0, 1][:, late * DEG:], RELU, bias=bias0[:])
        steps = []
        for piece, active in enumerate(actives):
            diff = sb.tile([P, n], F32, name="diff%d" % piece, tag=("rounded_n3", "diff1")[piece], align_bytes=64)
            nc.gpsimd.tensor_tensor(diff[:], active[:, 1, :], active[:, 0, :], ALU.subtract)
            step = sb.tile([P, n], F32, name="step%d" % piece)
            nc.scalar.activation(step[:], diff[:], RELU)
            steps.append(step)
        pair_max = [sb.tile([P, n], F32, name="pair_max%d" % piece) for piece in (0, 1)]
        for piece, active in enumerate(actives):
            nc.gpsimd.tensor_tensor(pair_max[piece][:], active[:, 0, :], steps[piece][:], ALU.add)

        best_first = sb.tile([P, GH], F32, name="best_first", align_bytes=64)
        best = placed.tile([P, 3 * G], F32, name="best", align_bytes=64, offset=at["n3"])
        result = sb.tile([P, 3 * G], F32, name="result", tag="rounded_n3", align_bytes=64)
        result0 = placed.tile([P, G], F32, name="result0", align_bytes=64, offset=at["n2"])

        group_max(best_first[:], banks[1, 0][:], DEG)
        group_max(best[:, GH:G], banks[1, 1][:], DEG)
        nc.scalar.activation(result[:, :GH], best_first[:], RELU, bias=bias123[:, 0:1])
        nc.sync.dma_start(out[P:2 * P, :GH], result[:, :GH])
        nc.scalar.activation(result[:, GH:G], best[:, GH:G], RELU, bias=bias123[:, 0:1])
        nc.sync.dma_start(out[P:2 * P, GH:], result[:, GH:G])
        for m in (2, 3):
            cols = slice((m - 1) * G, m * G)
            for e in (0, 1):
                if (m, e) != (2, 0):
                    multiply("n", m, e)
                multiply("c", m, e)
                group_max(best[:, cols][:, e * GH:(e + 1) * GH], banks[m, e][:], DEG)
            nc.scalar.activation(result[:, cols], best[:, cols], RELU, bias=bias123[:, m - 1:m])
            nc.sync.dma_start(out[m * P:(m + 1) * P, :], result[:, cols])
        group_max(result0[:, 2 * PIECE:], rest[:], DEG)
        for piece in (0, 1):
            group_max(result0[:, piece * PIECE:(piece + 1) * PIECE], pair_max[piece][:], DEG // 2)
        nc.sync.dma_start(out[:P, :], result0[:])
